import numpy as np, ml_dtypes
CORES = [8,136,40,168]
N = 4
BF = ml_dtypes.bfloat16
V, L, M, S, RO, E = 2048, 512, 8, 5, 2, 5
def pack(X, w, Q, T):
    return {"ent": np.ascontiguousarray(np.transpose(X, (0, 1, 3, 2)).reshape(N, 128, V)).astype(np.float32).astype(BF), "hw": np.reshape(w, (N, 128, 1)).astype(np.int32),
            "mix": np.reshape(Q, (N, 128, 16)).astype(np.float32).astype(BF), "goal": np.reshape(T, (N, 128, 1)).astype(np.int32)}
def genes(rng, p):
    return np.where(rng.random((N, 8, V, 16)) < p, rng.integers(1, 256, (N, 8, V, 16)), 0)
def aims(rng, Q):
    return np.matmul(rng.integers(1, 256, (N, 8, 1, 16)), Q)[:, :, 0]
def parts(rng):
    share = rng.choice(np.array([0.2, 0.3, 0.4, 0.55]), (N, 8, 1, 1))
    X = genes(rng, share * (0.5 + rng.random((N, 8, V, 1)))); w = rng.integers(1, 256, (N, 8, 16)); Q = rng.integers(-8, 9, (N, 8, 16, 16))
    return X, w, Q, aims(rng, Q)
def spot(x, w):
    u = np.matmul(x, w) & 4095
    return V // 2 + (((u * u >> 5) + 37 * u) & (V // 2 - 1))
def setup_inputs(rng):
    return pack(*parts(rng))
def setup_inputs_ends(rng):
    share = rng.choice(np.array([0.1, 0.2, 0.4, 0.7]), (N, 8, 1, 1)); share[:, 5] = 0.08; share[:, 6:] = 0.6
    X = 255 * (rng.random((N, 8, V, 16)) < share * (0.5 + rng.random((N, 8, V, 1)))).astype(np.int64)
    w = np.where(rng.random((N, 8, 16)) < 0.5, 1, 255)
    for g in (3, 6): w[:, g] = 255
    for g in (1, 7): w[:, g, :2] = 1; w[:, g, 2] = 255
    Q = 16 * rng.integers(0, 2, (N, 8, 16, 16)) - 8; Q[:, 5:] = 8
    T = 65280 * rng.integers(0, 2, (N, 8, 16)) - 32640; T[:, 5] = -32640
    T[1::2, 7] = -32640; T[0::2, 7] = 32640; T[1::2, 6] = 32640; T[0::2, 6] = -32640
    X[:, :, V - 1] = 255; X[:, :, V - 2] = 0
    for t in range(RO):
        for i in (0, 3, L - 1):
            for g in (1, 7): X[:, g, L * t + i] = 0; X[:, g, L * t + i, :3] = 255
            X[:, 6, L * t + i] = 255
        for i in (2, L - 2): X[:, 7, L * t + i] = 255; X[:, 6, L * t + i] = 0
    return pack(X, w, Q, T)
def setup_inputs_spread(rng):
    p = 1.3 * np.sqrt(rng.random((N, 8, V, 1))) * rng.random((N, 8, 1, 16))
    X = np.where(rng.random((N, 8, V, 16)) < p, np.minimum(np.exp2(8 * rng.random((N, 8, V, 16))).astype(np.int64), 255), 0)
    w = np.minimum(np.exp2(8 * rng.random((N, 8, 16))).astype(np.int64), 255)
    Q = rng.integers(-8, 9, (N, 8, 16, 16)) * (rng.random((N, 8, 16, 16)) < 0.2 + rng.random((N, 8, 16, 1)))
    T = np.clip(((2 * rng.random((N, 8, 16)) - 1) * np.exp2(10 + 5 * rng.random((N, 8, 16)))).astype(np.int64), -32640, 32640)
    return pack(X, w, Q, T)
def setup_inputs_corners(rng):
    X, w, Q, T = parts(rng); H = V // 2; full = rng.integers(1, 256, (N, 8, V, 16)); one = np.arange(16)[None, :] == rng.integers(0, 16, (H, 1))
    for r in range(N):
        for g in range(8):
            k = (g + r) % 8
            if k == 0: X[r, g] = full[r, g]
            if k == 1: X[r, g] = np.where(rng.random((V, 16)) < 0.02, full[r, g], 0)
            if k == 2: w[r, g] = 1
            if k == 3: w[r, g] = 255
            if k == 4: X[r, g, :H] = full[r, g, :H]; X[r, g, H:] = 0
            if k == 5: X[r, g, :H] = np.where(one, full[r, g, :H], 0); X[r, g, H:] = full[r, g, H:]
            if k == 6: Q[r, g] = 0; T[r, g] = 0
            if k == 7: X[r, g, :H, :8] = full[r, g, :H, :8]; X[r, g, :H, 8:] = 0; X[r, g, H:, :8] = 0; X[r, g, H:, 8:] = full[r, g, H:, 8:]
    return pack(X, w, Q, T)
def setup_inputs_alike(rng):
    X, w, Q, T = parts(rng); n = rng.choice(np.array([4, 12, 40]), (N, 8, 1)); n[:, 0] = 4; n[:, 1] = 40
    pick = (n * rng.random((N, 8, V))).astype(np.int64)
    return pack(np.take_along_axis(X[:, :, :40], np.minimum(pick, n - 1)[..., None], 2), w, Q, T)
def setup_inputs_close(rng):
    X, w, Q, T = parts(rng); H = V // 2; K = RO * L
    F = int(rng.integers(0, N)); Z = (F + 1) % N
    X[F] = rng.integers(1, 256, (8, V, 16))
    sub = np.zeros((16384, 16), np.int64); sub[:, 0] = 255; sub[:, 1:15] = 255 * ((np.arange(16384)[:, None] >> np.arange(14)[None, :]) & 1)
    for r in range(N):
        for g in range(8):
            s = int(rng.choice(np.array([-1, 1])))
            if g in (0, 7):
                Q[r, g, 0] = 0; Q[r, g, 0, 0] = -s; Q[r, g, 1:5] = -8 * s; Q[r, g, 5:] = s * rng.integers(0, 3, (11, 16)); T[r, g] = 32640 * s
            elif g in (1, 2):
                Q[r, g] = 8 * s; Q[r, g, 0, 1:] = 0; T[r, g] = 32640 * s; T[r, g, 0] = -32640 * s
            elif g == 3:
                z = rng.choice(np.array([-1, 1]), 16); Q[r, g] = 8 * z; T[r, g] = -32640 * z
            else:
                Q[r, g] = 8; T[r, g] = 32640
            if r == F: continue
            if g == 3:
                X[r, g, :K] = 255; X[r, g, :K, :15] -= rng.integers(0, 2, (K, 15))
                X[r, g, H:] = 254; X[r, g, H:, :15] -= rng.integers(0, 2, (H, 15))
                continue
            c = sub[15::16] if g in (0, 7) else sub
            X[r, g, H:] = 255; X[r, g, H:, 0] = 254 if g in (0, 7) else rng.integers(240 if g < 3 else 192, 255, H)
            if r == Z and g in (4, 5, 6):
                c = np.array(c); c[:, 0] = 254; X[r, g, H:, 0] = 255
            b = spot(c, w[r, g]); o = rng.permutation(np.unique(b, return_index=True)[1])
            e = np.concatenate([o, rng.choice(o[1:], L)])[:L]
            if g in (0, 7): e[0] = np.argmax(b)
            if g == 4: e[:] = e[0]
            if g == 6: e[L - 1] = e[0]
            X[r, g, :K] = c[rng.choice(o, K)]; X[r, g, :L] = c[e]
    return pack(X, w, Q, T)
def check_inputs(d):
    bad = []
    for k, lo, hi in (("ent", 0, 255), ("hw", 1, 255), ("mix", -8, 8), ("goal", -32640, 32640)):
        v = np.asarray(d[k]).astype(np.float64)
        if not np.all((v >= lo) & (v <= hi)): bad.append("range of " + k)
        elif np.any(v != np.floor(v)): bad.append("whole numbers of " + k)
    return bad
def reference(ent, hw, mix, goal):
    X = np.ascontiguousarray(np.transpose(np.asarray(ent).astype(np.float32).reshape(N, 8, 16, V), (0, 1, 3, 2)))
    w = hw.astype(np.float32).reshape(N, 8, 16, 1); Q = mix.astype(np.float32).reshape(N, 8, 16, 16); T = goal.astype(np.float32).reshape(N, 8, 1, 16)
    gr = np.arange(8)[:, None]; m = np.tile(np.arange(M), L); low = np.tri(L, L, -1, dtype=bool)
    def hash12(s, z): return np.matmul(z, w[s])[..., 0].astype(np.int64) & 4095
    def misfit(s, z): return np.add.reduce(np.abs(np.matmul(z, Q[s]) - T[s]), axis=-1)
    for t in range(RO):
        new = np.array(X)
        for r in range(N):
            q = (r + 1 + t % (N - 1)) % N
            A = X[r, :, L * t:L * t + L]; u = hash12(r, A)
            b = V // 2 + (((u * u >> 5) + 37 * u) & (V // 2 - 1)); B = X[r][gr, b]; AB = np.where(A == 0, B, A)
            first = np.logical_not(np.any((b[:, :, None] == b[:, None, :]) & low, axis=2))
            A2 = np.repeat(A, M, axis=1); B2 = np.repeat(B, M, axis=1); AB2 = np.repeat(AB, M, axis=1); c = np.zeros_like(A2)
            for d in range(S):
                v = hash12(q, np.where(c == 0, A2, c))
                h = ((v * v >> 5) + (2 * m + 1) * v + 811 * d) & (V - 1)
                p = X[q][gr, h]; c = np.where(c == 0, p, c)
            fa, fb, fab = [misfit(q, np.where(e == 0, c, e)) for e in (A2, B2, AB2)]
            count = np.add.reduce((fab > np.minimum(fa, fb)).reshape(8, L, M).astype(np.int64), axis=2)
            donor = p.reshape(8, L, M, 16)[:, :, 0]
            ga, la = np.nonzero((count <= E + (u & 1)) & first); ba = b[ga, la]
            new[r, ga, L * t + la] = AB[ga, la]; new[r, ga, ba] = donor[ga, la]
        X = new
    return {"y": np.ascontiguousarray(np.transpose(X, (0, 1, 3, 2))).reshape(N, 128, V).astype(BF)}

@@ -1,0 +1,614 @@
+from concourse.bass import DstId, RemoteDMATransfer
+from concourse.mybir import dt, AluOpType as ALU, AxisListType, ActivationFunctionType as ACT
+
+BF, F32, F16, I32, U16 = "bfloat16", "float32", "float16", "int32", "uint16"
+SB = {
+    "raw": (2560, BF), "t0": (2560, F32), "t1": (2048, F32), "t2": (2048, F32), "t3": (2048, F32),
+    "e": (4096, F16), "rr": (4096, BF), "sg": (2048, BF),
+    "ain0": (512, BF), "ain1": (512, BF), "a2e": (2048, BF), "ya": (512, BF),
+    "bg0": (1024, BF), "bg1": (1536, BF), "bgin0": (1024, BF), "bgin1": (1024, BF), "gw": (1024, F32),
+    "don0": (512, F32), "don1": (512, BF), "donin0": (512, F32), "donin1": (512, BF),
+    "cnt0": (64, BF), "cnt1": (64, BF), "cntin0": (64, BF), "cntin1": (64, BF),
+    "zao": (1024, BF), "zaj": (1024, BF), "zb": (512, BF), "m2": (512, BF), "zab": (512, BF),
+    "xb": (1536, BF), "yy": (1536, BF), "c2": (1536, BF), "ab": (4608, F32), "nk": (128, BF), "pk": (128, BF), "k8": (128, BF),
+    "cw": (32, F32), "nt": (64, F32), "q5": (384, F32),
+    "fl": (512, BF), "ob": (256, BF),
+    "hwi": (1, I32), "gli": (1, I32), "mx": (16, BF), "wf": (4, F32), "wi": (2, I32),
+    "one": (128, BF), "idn": (128, BF), "nid": (128, BF), "blk": (128, BF), "upp": (128, BF), "b8": (8, F32), "b8a": (8, F32),
+    "qq": (128, BF), "nq": (128, BF), "wp": (144, BF), "sp": (144, BF), "fp": (144, BF), "w8": (16, BF),
+    "sm": (48, F32), "cm": (128, BF), "xp": (2, I32),
+    "x16": (16, I32), "x15": (16, I32), "x3": (8, I32), "e16": (16, F32), "e4": (4, F32), "pc": (4, F32),
+    "ct": (1280, F32),
+    "ch": (512, BF), "dum": (64, F32), "du0": (64, F32), "base": (64, F32), "la0": (32, F32), "dif": (128, F32), "thr": (128, F32),
+    "q4": (384, F32), "ss": (384, F32), "sq": (576, F32), "ni": (576, I32), "hi": (576, I32), "off": (576, U16),
+    "boff": (64, U16), "soff": (64, U16), "uoff": (64, U16),
+    "bv": (64, F16), "bm": (1024, F16), "eq": (1536, BF), "sf": (64, F32), "nd": (64, F32), "pi": (64, I32), "pj": (64, I32),
+    "tp": (64, F32), "ff": (32, F32), "ft0": (1056, BF), "ft1": (1056, BF), "fg": (512, BF), "ac": (64, F32), "ad": (64, F32), "ae": (64, F32),
+}
+BANKS = ["h0", "h1", "p0", "p1", "u0", "u1", "u2", "dd"]
+SCRATCH = {k: ("sbuf", [128, v[0]], v[1]) for k, v in SB.items()}
+SZ = [2, 2, 2, 2]
+
+
+def chunks(sz):
+    SZ[:] = sz
+    for c, n in enumerate(sz):
+        SB["hz%d" % c] = (144, F16)
+        SCRATCH["hz%d" % c] = ("sbuf", [128, 36 // n, 4 * n], F16)
+
+
+chunks(list(SZ))
+for _b in BANKS:
+    SCRATCH[_b] = ("psum", [128, 512], F32)
+DMAS = ["la0", "la1", "lb", "lhw", "lgl", "lmx", "y0", "y1", "y2", "y3", "lw", "lg"]
+SENDS = ["a0", "a1", "bg0", "bg1", "don0", "don1", "cnt0", "cnt1"]
+SEMAPHORES = ["eV", "eS", "eP", "eG"] + ["d_" + k for k in DMAS] + ["r_" + k for k in SENDS] + ["l_" + k for k in SENDS]
+
+PAR = {"sig": [0, 1.24, 1.91, 3.56], "look": 100.0, "w": 300.0, "ns": [1, 1, 1, 1, 1, 1, 2, 2], "k5v": [0, 0, 0, 0], "vo": 4.13,
+       "vd": 0.3, "pa": 1.25, "ma": 3.5, "f0": 1.8, "hs": 0, "h3": 0, "o1": 0, "xs": [0, 1, 0, 1, 1, 1, 1, 1], "es": 1,
+       "pro": 4.65, "f1": 9.06}
+NUDGE = {3: -2, 12: 4, 19: 8, 21: -1, 23: -4, 31: 2, 35: 8, 48: 8, 53: 4, 59: -2, 78: 5, 81: 6, 86: -1, 87: 4, 88: 8, 89: 4, 90: 6, 91: 5, 92: -2, 93: -8, 95: 1, 114: 1, 117: 2, 119: -8, 121: 4, 127: 4, 136: -6, 147: -2, 150: -8, 154: -8, 157: -1, 162: 2, 179: -1, 195: 1, 208: -8, 214: 6, 215: 12, 216: 1, 243: -4, 250: 8, 254: 8, 268: -1, 275: -1, 279: -8, 295: -2, 302: -2, 304: 2, 305: -8, 309: -1, 331: -2, 347: 4, 350: -2, 352: -1, 363: -4, 364: -8, 369: -8, 372: 1, 377: -2, 389: -2, 403: 2, 413: -4, 437: 1, 442: -1, 456: 1, 457: -1, 458: -4, 466: 8, 472: 2, 476: 2, 495: 2, 496: 2, 500: 1, 523: -8, 527: 3, 531: 2, 539: -4, 540: -4, 564: 4, 566: 2, 567: 2, 568: 2, 571: 8, 588: 1, 594: -1, 598: 2, 602: 8, 604: -4, 610: -5, 619: 1, 638: -2, 645: 2, 646: 8, 648: -8, 660: -2, 664: -1, 667: -8, 681: -1, 689: 8, 690: 2, 695: -1, 697: -8, 704: -1, 727: 8, 731: 2, 734: 4, 738: -8, 741: 2, 742: 8, 751: -8, 768: -1, 774: 2, 777: -8, 781: 4, 782: 1, 788: 4, 793: -4, 795: -4, 798: 4, 800: -6, 802: 1, 810: 6, 814: -4, 815: -2, 820: 1, 831: 4, 839: -8, 845: 1, 847: 1, 849: 1, 853: -2, 854: 1, 857: 4, 864: 2, 866: 1, 874: -1, 886: -1, 887: 2, 891: 1, 892: 4, 903: 4, 915: 1, 922: 8, 923: 2, 924: 2, 936: -2, 980: -4, 981: 4, 983: 1, 986: -2, 993: 8, 996: -1, 997: -2, 1014: 2, 1018: 4, 1020: 8, 1022: 1, 1031: 8, 1032: -4}
+MAGIC = float(3 * 2 ** 34)
+CV, CP, GA, SC, LAT = 1.0, 0.5, 1.5, 3.5, 150.0
+
+
+def R(name, lo=0, hi=None, st=1):
+    return (name, lo, SB[name][0] if hi is None and name in SB else (512 if hi is None else hi), st)
+
+
+def IND(win, off):
+    return ("ind", win, off)
+
+
+def n_of(a):
+    if a[0] == "ind":
+        return 16 * n_of(a[2])
+    return (a[2] - a[1] + a[3] - 1) // a[3]
+
+
+def two(a):
+    return a[0] in SB and SB[a[0]][1] in (BF, F16, U16)
+
+
+def ap(T, a):
+    if not isinstance(a, tuple):
+        return a
+    if a[0] == "ind":
+        return ap(T, a[1]).indirect(ap(T, a[2]))
+    if a[0][:2] == "hz":
+        w = SCRATCH[a[0]][1][2]
+        return T[a[0]][:, a[1] // w:a[2] // w:a[3], :]
+    if a[3] == 1:
+        return T[a[0]][:, a[1]:a[2]]
+    return T[a[0]][:, a[1]:a[2]:a[3]]
+
+
+def parts(a):
+    if not isinstance(a, tuple):
+        return []
+    if a[0] == "ind":
+        return [a[1], a[2]]
+    return [a]
+
+
+def build():
+    ops = []
+    pr = [0.0]
+    sz = SZ
+    m0 = [sum(sz[:c]) for c in range(len(sz))]
+
+    def add(eng, fn, rd, wr, cost, kind="c", name=None, lat=0.0):
+        r2 = [x for a in rd for x in parts(a)]
+        w2 = []
+        for a in wr:
+            if a[0] == "ind":
+                w2.append(a[1]); r2.append(a[2])
+            else:
+                w2.append(a)
+        ops.append({"eng": eng, "fn": fn, "rd": r2, "wr": w2, "cost": cost, "kind": kind, "name": name, "prio": pr[0], "lat": lat})
+
+    def vcost(out, ins, base):
+        n = n_of(out)
+        if out[0] == "ind":
+            return 50 + CV * SC * n
+        if ins[0][0] == "ind":
+            return 50 + CV * GA * n
+        return CV * max(64, base * n)
+
+    def cp_(out, a):
+        add("V", lambda g, T: g.vector.tensor_copy(ap(T, out), ap(T, a)), [a], [out],
+            vcost(out, [a], 0.5 if a[0] != "ind" and out[0] != "ind" and two(a) and two(out) else 1))
+
+    def ts(out, a, s1, op0, s2=None, op1=None):
+        def fn(g, T):
+            if op1 is None:
+                return g.vector.tensor_scalar(ap(T, out), ap(T, a), ap(T, s1), None, op0)
+            return g.vector.tensor_scalar(ap(T, out), ap(T, a), ap(T, s1), ap(T, s2), op0, op1)
+        add("V", fn, [a, s1, s2], [out], vcost(out, [a], 0.5 if two(a) and two(out) else 1))
+
+    def tt(out, a, b, op):
+        add("V", lambda g, T: g.vector.tensor_tensor(ap(T, out), ap(T, a), ap(T, b), op), [a, b], [out],
+            vcost(out, [a], 1 if a[0] in BANKS or b[0] in BANKS else 2))
+
+    def ms(out, c):
+        add("V", lambda g, T: g.vector.memset(ap(T, out), c), [], [out], CV * max(64, n_of(out) * (0.5 if two(out) else 1)))
+
+    def act(out, a, f, bias=0.0, scale=1.0):
+        add("S", lambda g, T: g.scalar.activation(ap(T, out), ap(T, a), f, bias=ap(T, bias), scale=ap(T, scale)), [a, bias, scale], [out],
+            (65 + CV * GA * n_of(out)) if a[0] == "ind" else CV * max(64, n_of(out)))
+
+    def mm(lst, start=True, stop=True):
+        def fn(g, T):
+            ins = None
+            for i, (o, l, r) in enumerate(lst):
+                ins = g.tensor.matmul(ap(T, o), ap(T, l), ap(T, r), start and i == 0, stop and i == len(lst) - 1)
+            return ins
+        c = sum(max(min(64, n_of(l)), n_of(r)) * (4 if SB[l[0]][1] == F32 else 1) for o, l, r in lst)
+        add("P", fn, [x for o, l, r in lst for x in (l, r)], [o for o, l, r in lst], CP * c)
+
+    def iota(out, pat, base, cm=0):
+        if SB[out[0]][1] == I32:
+            add("G", lambda g, T: g.iota(ap(T, out), pat, base, cm), [], [out], 130 + 2 * CV * n_of(out))
+        else:
+            add("G", lambda g, T: g.iota(ap(T, out), pat, base, cm, allow_small_or_imprecise_dtypes=True), [], [out], 130 + 2 * CV * n_of(out))
+
+    def sel(out, a, pat, op, base, cm):
+        add("G", lambda g, T: g.affine_select(ap(T, out), ap(T, a), pat, op, 0.0, base, cm), [a], [out], 170 + 2 * CV * n_of(out))
+
+    def load(eng, name, out, src):
+        def fn(g, T):
+            q = g.sync if eng == "Y" else g.scalar
+            return q.dma_start(ap(T, out), src(T))
+        add(eng, fn, [], [out], 100, "dma", name, 2000 + n_of(out) * 1.5)
+
+    def store(eng, name, a, at=None):
+        at = a[1] if at is None else at
+
+        def fn(g, T):
+            q = g.sync if eng == "Y" else g.scalar
+            return q.dma_start(T.y[:, at:at + n_of(a)], ap(T, a))
+        add(eng, fn, [a], [], 100, "dma", name, 2000 + n_of(a) * 1.5)
+
+    def send(name, src, dst, hop):
+        add("G", (src, dst, hop), [src], [dst], 1000, "send", name, 2500 + n_of(src) * (2 if two(src) else 4) * 128 / 40.0)
+
+    pr[0] = -10
+    load("Y", "la0", R("raw", 0, 512), lambda T: T.ent[:, 0:512])
+    load("S", "lb", R("raw", 1024, 2048), lambda T: T.ent[:, 1024:2048])
+    load("Y", "lhw", R("hwi"), lambda T: T.hw[:])
+    load("Y", "la1", R("raw", 512, 1024), lambda T: T.ent[:, 512:1024])
+    load("S", "lmx", R("mx"), lambda T: T.mix[:])
+    load("Y", "lgl", R("gli"), lambda T: T.goal[:])
+    send("a0", R("raw", 0, 512), R("ain0"), 1)
+    pr[0] = -9
+    ms(R("one"), 1.0)
+    iota(R("x16"), [[-1, 16]], 16, 1)
+    sel(R("b8a"), R("one", 0, 8), [[-16, 8]], ALU.is_ge, 0, 1)
+    sel(R("b8"), R("b8a"), [[16, 8]], ALU.is_ge, 15, -1)
+    sel(R("idn"), R("one"), [[-1, 128]], ALU.is_equal, 0, 1)
+    for k in ("wp", "sp", "fp"):
+        ms(R(k), 0.0)
+    ms(R("cm"), -2048.0)
+    ts(R("x15"), R("x16"), 15, ALU.bitwise_and)
+    ts(R("x3", 0, 4), R("x16", 0, 4), 3, ALU.bitwise_and)
+    ts(R("e16"), R("x15"), 0.0, ALU.is_equal)
+    ts(R("e4"), R("x3", 0, 4), 0.0, ALU.is_equal)
+    cp_(R("pc", 0, 1), R("x15", 0, 1))
+    ts(R("nid"), R("idn"), -1.0, ALU.mult)
+    cp_(R("wf", 0, 1), R("hwi"))
+    ts(R("wi", 0, 1), R("hwi"), 15, ALU.bitwise_and)
+    cp_(R("wf", 1, 2), R("wi", 0, 1))
+    ts(R("wp", 15, 143, 16), R("b8"), R("wf", 0, 1), ALU.mult)
+    ts(R("w8", 0, 8), R("b8"), R("wf", 0, 1), ALU.mult)
+    ts(R("w8", 8, 16), R("b8"), R("wf", 1, 2), ALU.mult, -256.0, ALU.mult)
+    nc = len(sz)
+    for m in range(8):
+        act(R("ct", 32 * m, 32 * m + 32), R("one", 0, 32), ACT.Identity, scale=-256.0 * (2 * m + 1) ** 2)
+    for d in range(1, 5):
+        act(R("ct", 256 * d, 256 * d + 256), R("ct", 0, 256), ACT.Identity, bias=32.0 * 811 * d)
+    for a in range(8):
+        act(R("blk", 16 * a, 16 * a + 16), R("one", 0, 16), ACT.Identity, scale=R("b8", a, a + 1))
+    pr[0] = -8
+    tb = ["p0", "p1", "u0", "u1"]
+    for k in (0, 2, 3, 1):
+        lo = 512 * k
+        ts(R("sg", lo, lo + 512), R("raw", lo, lo + 512), 0.0, ALU.is_gt, 2048.0, ALU.mult)
+        mm([(R(tb[k]), R("idn"), R("raw", lo, lo + 512)), (R(tb[k]), R("idn"), R("sg", lo, lo + 512))])
+        act(R("t0", lo, lo + 512), R(tb[k]), ACT.Identity, bias=-1024.0)
+    pr[0] = -7
+    send("a1", R("raw", 512, 1024), R("ain1"), 2)
+    for c in range(nc):
+        if sz[c] < 4:
+            ts(R("hz%d" % c, 0, 144), R("wp", 0, 144), 0.0, ALU.mult)
+    sel(R("upp"), R("blk"), [[1, 128]], ALU.is_gt, 0, -1)
+    iota(R("du0"), [[0, 32], [16, 2]], 1025)
+    iota(R("la0"), [[16, 32]], 0)
+    iota(R("ch"), [[1, 16], [0, 32]], 0)
+    iota(R("ft0"), [[0, 1056]], 0)
+
+    def index_chain(bank, o, beta, w=64):
+        if PAR["o1"]:
+            act(R("q5", o, o + w), R(bank, 0, w), ACT.Identity, bias=MAGIC)
+            act(R("q4", o, o + w), R("q5", o, o + w), ACT.Identity, bias=-MAGIC)
+        else:
+            ts(R("q4", o, o + w), R(bank, 0, w), MAGIC, ALU.add, MAGIC, ALU.subtract)
+        tt(R("ss", o, o + w), R(bank, 0, w), R("q4", o, o + w), ALU.subtract)
+        act(R("sq", o, o + w), R("ss", o, o + w), ACT.Square, bias=beta)
+
+    pr[0] = -6
+    mm([(R("h1", 0, 64), R("idn"), R("cm", 0, 64))] + [(R("h1", 0, 64), R("wp", 15 - r, 143 - r), R("raw", r, 1024, 16)) for r in range(16)])
+    index_chain("h1", 256, 2048.0 + 592)
+    ts(R("ni", 256, 320), R("sq", 256, 320), -592.0 * 592, ALU.add)
+    ts(R("hi", 256, 320), R("ni", 256, 320), 5, ALU.arith_shift_right, 1023, ALU.bitwise_and)
+    cp_(R("boff"), R("hi", 256, 320))
+    ts(R("bv"), R("hi", 256, 320), 1.0, ALU.add)
+    pr[0] = 2.0
+    for r in range(16):
+        ts(R("bm", 64 * r, 64 * r + 64), R("bv"), R("e16", r, r + 1), ALU.mult)
+    for k, b in enumerate(("u2", "dd")):
+        mm([(R(b), R("upp"), R("bm", 512 * k, 512 * k + 512))] + [(R(b, 64 * r, 64 * r + 64), R("nid"), R("bv")) for r in range(8)])
+        ts(R("eq", 512 * k, 512 * k + 512), R(b), 0.0, ALU.is_equal, 2048.0, ALU.mult)
+    mm([(R("u2"), R("blk"), R("bm", 0, 1024, 2))] + [(R("u2", 32 * r, 32 * r + 32), R("nid"), R("bv", 1, 64, 2)) for r in range(16)])
+    ts(R("eq", 1024, 1536), R("u2"), 0.0, ALU.is_equal, 2048.0, ALU.mult)
+    mm([(R("dd", 0, 64), R("idn"), R("bv"))] + [(R("dd", 0, 64), R("idn"), R("eq", 64 * r, 64 * r + 64)) for r in range(16)]
+       + [(R("dd", 1, 64, 2), R("idn"), R("eq", 1024 + 32 * r, 1056 + 32 * r)) for r in range(16)])
+    ts(R("dum"), R("du0"), R("pc", 0, 1), ALU.add)
+    tt(R("sf"), R("dd", 0, 64), R("dum"), ALU.min)
+    ts(R("soff"), R("sf"), -1.0, ALU.add)
+    ts(R("nd"), R("sf"), 1024.5, ALU.is_lt)
+    ts(R("pi"), R("ss", 256, 320), 2048.0, ALU.add)
+    ts(R("pj"), R("pi"), 1, ALU.bitwise_and)
+    ts(R("tp"), R("pj"), 5.5, ALU.add)
+    tt(R("nt"), R("tp"), R("nd"), ALU.mult)
+    ts(R("base", 0, 32), R("la0"), R("pc", 0, 1), ALU.add, 1024.0, ALU.add)
+    ts(R("base", 32, 64), R("base", 0, 32), -512.0, ALU.add)
+    for t in range(2):
+        tt(R("dif", 64 * t, 64 * t + 32), R("hi", 256 + 32 * t, 288 + 32 * t), R("base", 0, 32), ALU.subtract)
+        ms(R("dif", 64 * t + 32, 64 * t + 64), -512.0)
+    cp_(R("sp", 15, 143, 16), R("b8"))
+    pr[0] = 3.0
+    iota(R("ft1"), [[0, 1056]], 0)
+    iota(R("t0", 2048, 2560), [[0, 512]], 0)
+    iota(R("raw", 2048, 2560), [[0, 512]], 0)
+    add("Y", lambda g, T: g.sync.dma_start(T.gw[:, 512:1024], T.t0[:, 0:512]), [R("t0", 0, 512)], [R("gw", 512, 1024)], 100, "dma", "lg", 3500)
+    load("Y", "lw", R("bg1", 1024, 1536), lambda T: T.ent[:, 512:1024])
+    for a in range(8):
+        act(R("qq", 16 * a, 16 * a + 16), R("mx"), ACT.Identity, scale=R("b8", a, a + 1))
+    act(R("nk"), R("idn"), ACT.Identity, scale=-256.0)
+    act(R("pk"), R("idn"), ACT.Identity, scale=256.0)
+    act(R("k8"), R("idn"), ACT.Identity, scale=2048.0)
+    iota(R("cw"), [[16, 16], [0, 2]], 0)
+    ts(R("wf", 2, 3), R("gli"), -1.0, ALU.mult)
+    ms(R("sm"), 0.0)
+    for lo, s in ((0, 1.0), (8, 1.0), (16, -1.0), (40, -1.0)):
+        ts(R("sm", lo, lo + 8), R("b8"), s, ALU.mult)
+    for b in range(4):
+        ts(R("fp", 12 + b, 140 + b, 16), R("b8"), R("e4", b, b + 1), ALU.mult)
+
+    def first_lanes(t, bank):
+        ft = "ft%d" % t
+        for k in range(15, -1, -1):
+            cp_(IND(R(ft), R("soff", 32 * t + 2 * k, 32 * t + 2 * k + 2)), R("ch", 32 * k, 32 * k + 32))
+        act(R("fg"), IND(R(ft), R("boff", 32 * t, 32 * t + 32)), ACT.Copy)
+        mm([(R(bank, 0, 32), R("sp", 15 - r, 143 - r), R("fg", r, 512, 16)) for r in range(16)])
+        tt(R("ff"), R(bank, 0, 32), R("cw"), ALU.is_equal)
+        for k in range(2):
+            tt(R("thr", 64 * t + 32 * k, 64 * t + 32 * k + 32), R("ff"), R("nt", 32 * t, 32 * t + 32), ALU.mult)
+
+    pr[0] = PAR["f0"]
+    first_lanes(0, "dd")
+    tabs = ["t0", "t1", "t2", "t3", "raw"]
+
+    def to_offsets(bank, d, col, o, w):
+        tt(R("ni", o, o + w), R(bank, 256, 256 + w), R("ct", 256 * d + col, 256 * d + col + w), ALU.add)
+        ts(R("hi", o, o + w), R("ni", o, o + w), 5, ALU.arith_shift_right, 2047, ALU.bitwise_and)
+        cp_(R("off", o, o + w), R("hi", o, o + w))
+
+    def prologue(t):
+        ain, o = "ain%d" % t, 320 * t
+        mm([(R("h0", 0, 32), R("idn"), R("cm", 0, 32))] + [(R("h0", 0, 32), R("wp", 15 - r, 143 - r), R(ain, r, 512, 16)) for r in range(16)])
+        ts(R("q4", o, o + 32), R("h0", 0, 32), MAGIC, ALU.add, MAGIC, ALU.subtract)
+        tt(R("ss", o, o + 32), R("h0", 0, 32), R("q4", o, o + 32), ALU.subtract)
+        act(R("a2e", 512 * t, 512 * t + 512), R(ain), ACT.Identity, bias=-256.0)
+        for c in range(2):
+            for k in range(4):
+                act(R("h%d" % c, 256 + 32 * k, 288 + 32 * k), R("ss", o, o + 32), ACT.Square, bias=2064.0 + 32 * (4 * c + k))
+            to_offsets("h%d" % c, 0, 128 * c, o + 128 * c, 128)
+        act(R("zao", 512 * t, 512 * t + 512), R("raw", 512 * t, 512 * t + 512), ACT.Relu, bias=1.0, scale=-1.0)
+        act(R("zaj", 512 * t, 512 * t + 512), R(ain), ACT.Relu, bias=1.0, scale=-1.0)
+
+    nblk = [0]
+    nu = [0]
+    for t in range(2):
+        P0 = 100.0 * t
+        ain, bg, bgin = "ain%d" % t, "bg%d" % t, "bgin%d" % t
+        zao, zaj = R("zao", 512 * t, 512 * t + 512), R("zaj", 512 * t, 512 * t + 512)
+        bo = R("boff", 32 * t, 32 * t + 32)
+        if t == 0:
+            pr[0] = -5
+            prologue(0)
+        else:
+            pr[0] = 40
+            tt(R("ac"), R("cntin0"), R("thr", 0, 64), ALU.is_lt)
+            tt(R("ad"), R("ac"), R("dif", 0, 64), ALU.mult)
+            tt(R("ae"), R("ad"), R("base"), ALU.add)
+            cp_(R("uoff"), R("ae"))
+            cp_(IND(R("t0", 1024, 2560), R("uoff", 0, 32)), R("donin0"))
+            act(R("t0", 0, 512), IND(R("gw"), R("uoff", 32, 64)), ACT.Copy)
+        spans = [(0, 2048)] if t == 0 else [(1024, 2048), (0, 512)]
+        ev = []
+        left = [2048, 2048]
+
+        def tables(d):
+            for lo, hi in spans:
+                if d < 4:
+                    act(R(tabs[d], lo, hi), R("t0", lo, hi), ACT.Identity, bias=-256.0 * d)
+                else:
+                    act(R("raw", lo, hi), R("t0", lo, hi), ACT.Relu, bias=-1024.0)
+
+        def partners():
+            act(R(bg, 0, 512), IND(R("raw", 1024, 2048), bo), ACT.Copy)
+            mm([(R("p0"), R("idn"), R(bg, 0, 512)), (R("p0"), R("pk"), zao)])
+            act(R("ya"), R("p0"), ACT.Relu, bias=-256.0)
+            mm([(R("p1"), R("idn"), R("raw", 512 * t, 512 * t + 512)), (R("p1"), R("idn"), R("ya"))])
+            act(R(bg, 512, 1024), R("p1"), ACT.Identity)
+            send(bg, R(bg, 0, 1024), R(bgin), 1 + t)
+            if t == 0:
+                act(R("ya"), R(bg, 512, 1024), ACT.Sign)
+                mm([(R("p1"), R("idn"), R(bg, 512, 1024)), (R("p1"), R("k8"), R("ya"))])
+                act(R("gw", 0, 512), R("p1"), ACT.Identity, bias=-1024.0)
+
+        def masks():
+            act(R("zb"), R(bgin, 0, 512), ACT.Relu, bias=1.0, scale=-1.0)
+            act(R("zab"), R(bgin, 512, 1024), ACT.Relu, bias=1.0, scale=-1.0)
+
+        def step(c, d):
+            n, o = sz[c], 32 * m0[c]
+            lo, hi = 512 * m0[c], 512 * (m0[c] + n)
+            rr = R("rr", lo, hi)
+            if d == 4 and c == 0:
+                act(R("don%d" % t), IND(R("t0" if t == 0 else "raw", 0, 2048), R("off", 0, 32)), ACT.Copy)
+                send("don%d" % t, R("don%d" % t), R("donin%d" % t), -1 - t)
+            w = 256 if PAR["hs"] else 512
+            oo = o + (320 * t if d == 0 else 0)
+            for k in range(512 * n // w):
+                ek = R("e", lo + w * k, lo + w * k + w)
+                al = 512 * t + w * k % 512
+                tt(ek, IND(R(tabs[d], 0, 2048), R("off", oo + w * k // 16, oo + (w * k + w) // 16)), R("a2e", al, al + w) if d == 0 else ek, ALU.max)
+                if d < 4 and (w * k + w) % 512 == 0:
+                    act(R("rr", ek[2] - 512, ek[2]), R("e", ek[2] - 512, ek[2]), ACT.Identity, bias=144.0 - 127.5 / 256, scale=1.0 / 256)
+            if d == 4:
+                return
+            bank, st, w = ["h0", "h1", "u2"][c % (2 + PAR["h3"])], 4 * n, 32 * n
+            me = [(R(bank, 0, w), R("idn"), R("cm", 0, w))] + [(R(bank, r, w, st), R("e", lo + r, hi, st), R("w8", 0, 8)) for r in range(st)]
+            mr = [(R(bank, r, w, st), R("rr", lo + r, hi, st), R("w8", 8, 16)) for r in range(st)]
+            if PAR["es"]:
+                mm(me, stop=False)
+                mm(mr, start=False)
+            else:
+                mm(me + mr)
+            hz, rep = "hz%d" % c, 4 // n
+            ts(R("q4", o, o + w), R(bank, 0, w), MAGIC, ALU.add, MAGIC, ALU.subtract)
+            tt(R(hz, 16 - st, 144 - st, rep), R(bank, 0, w), R("q4", o, o + w), ALU.subtract)
+            mm([(R(bank, 128, 128 + w), R(hz, 16 - st - st * k, 144 - st - st * k), R("idn", k, 128, rep)) for k in range(rep)])
+            for k in range(n):
+                act(R(bank, 256 + 32 * k, 288 + 32 * k), R(bank, 128 + 32 * k, 160 + 32 * k), ACT.Square, bias=2064.0 + 32 * (m0[c] + k))
+            to_offsets(bank, d + 1, o, o, w)
+            if d == 3:
+                if PAR["k5v"][c]:
+                    ts(rr, rr, -144.0, ALU.add, 0.0, ALU.max)
+                else:
+                    act(rr, rr, ACT.Relu, bias=-144.0)
+
+        def verdict(c, mb, s, ns):
+            k = nblk[0]; nblk[0] += 1
+            m, w = m0[c] + mb, 512 // ns
+            pb, ub, o = R("p%d" % (k % 2), 0, w), R("u%d" % (k % 3), 0, w), 512 * (k % 3)
+            ao = 1536 * (k % 3)
+            xb, yy, c2 = R("xb", o, o + w), R("yy", o, o + w), R("c2", o, o + w)
+            mm([(pb, R("idn"), R("e", 512 * m + s, 512 * m + 512, ns)), (pb, R("nk"), R("rr", 512 * m + s, 512 * m + 512, ns))])
+            q, nq = R("qq"), R("nq")
+            lanes = [R(bgin, s, 512, ns), R(ain, s, 512, ns), R(bgin, 512 + s, 1024, ns)]
+            tt(xb, pb, R("zb", s, 512, ns), ALU.mult)
+            za = R("zaj", 512 * t + s, 512 * t + 512, ns)
+            tt(yy, pb, za, ALU.mult)
+            if PAR["xs"][m]:
+                tt(c2, pb, R("zab", s, 512, ns), ALU.mult)
+            else:
+                pb = R("u%d" % (nu[0] % (3 - PAR["h3"])), 0, w); nu[0] += 1
+                mm([(pb, R("idn"), xb), (pb, R("pk"), za)])
+                act(c2, pb, ACT.Relu, bias=-256.0)
+            for x in range(3):
+                ub = R("u%d" % (nu[0] % (3 - PAR["h3"])), 0, w); nu[0] += 1
+                mm([(ub, q, lanes[x]), (ub, q, (xb, yy, c2)[x])])
+                act(R("ab", ao + 512 * x, ao + 512 * x + w), ub, ACT.Abs, bias=R("wf", 2, 3))
+            half, ml = m // 4, m % 4
+            for b in range(4 // ns):
+                out = R("dd", 256 * half + 4 * ml + s + ns * b, 256 * half + 256, 16)
+                mm([(out, R("ab", ao + 512 * x + b, ao + 512 * x + w, 4 // ns), R("sm", 32 - 16 * x, 48 - 16 * x)) for x in range(3)])
+            left[half] -= w
+            if left[half] == 0:
+                o = 256 * half
+                if left[1 - half]:
+                    act(R("fl", o, o + 256), R("dd", o, o + 256), ACT.Relu)
+                else:
+                    ts(R("fl", o, o + 256), R("dd", o, o + 256), 0.0, ALU.max)
+                mm([(R("h0", 256, 384), R("fl", o + 128 * x, o + 128 * x + 128), R("idn")) for x in range(2)])
+                act(R("ob", 128 * half, 128 * half + 128), R("h0", 256, 384), ACT.Sign)
+
+        for d in range(1, 4):
+            ev.append((d - 1.01, lambda d=d: tables(d)))
+        if t == 1:
+            ev.append((0.5, lambda: (tables(4), store("Y", "y0", R("raw", 0, 512)))))
+        if t == 0:
+            ev.append((PAR["pro"], lambda: prologue(1)))
+            ev.append((PAR["f1"], lambda: first_lanes(1, "h1")))
+        ev.append((PAR["pa"], partners))
+        ev.append((PAR["ma"], masks))
+        for c in range(len(sz)):
+            for d in range(5):
+                ev.append((d + PAR["sig"][c], lambda c=c, d=d: step(c, d)))
+            for mb in range(sz[c]):
+                ns = PAR["ns"][m0[c] + mb]
+                for s in range(ns):
+                    ev.append((PAR["vo"] + PAR["sig"][c] + PAR["vd"] * (mb + s / ns), lambda c=c, mb=mb, s=s, ns=ns: verdict(c, mb, s, ns)))
+        ev.sort(key=lambda x: x[0])
+        for v, f in ev:
+            pr[0] = P0 + v
+            f()
+        pr[0] = P0 + 20
+        for k in range(2):
+            mm([(R("h1", 32 * k, 32 * k + 32), R("fp", 12 - 4 * r, 140 - 4 * r), R("ob", 128 * x + r, 128 * x + 128, 4)) for x in range(2) for r in range(4)])
+        act(R("cnt%d" % t), R("h1", 0, 64), ACT.Identity)
+        send("cnt%d" % t, R("cnt%d" % t), R("cntin%d" % t), -1 - t)
+    pr[0] = 140
+    tt(R("ac"), R("cntin1"), R("thr", 64, 128), ALU.is_lt)
+    tt(R("ad"), R("ac"), R("dif", 64, 128), ALU.mult)
+    tt(R("ae"), R("ad"), R("base"), ALU.add)
+    cp_(R("uoff"), R("ae"))
+    cp_(IND(R("raw", 1024, 2560), R("uoff", 0, 32)), R("donin1"))
+    act(R("ya"), IND(R("bg1", 512, 1536), R("uoff", 32, 64)), ACT.Copy)
+    store("S", "y1", R("ya"), 512)
+    store("Y", "y2", R("raw", 1024, 1536))
+    store("S", "y3", R("raw", 1536, 2048))
+    return ops
+
+
+def schedule(ops):
+    hist = {}
+    for i, o in enumerate(ops):
+        if "deps" in o:
+            break
+        deps = {}
+        hard = set()
+        acc = [(a, False) for a in o["rd"]] + [(a, True) for a in o["wr"]]
+        for a, w in acc:
+            bank = a[0] in BANKS
+            for j, lo, hi, wj in hist.get(a[0], []):
+                if j == i:
+                    continue
+                if bank:
+                    deps[j] = deps.get(j, False) or (wj and not w)
+                elif lo < a[2] and a[1] < hi and (w or wj):
+                    deps[j] = deps.get(j, False) or (wj and not w)
+                    hard.add(j)
+        o["hard"] = hard
+        for a, w in acc:
+            h = hist.setdefault(a[0], [])
+            if a[0] in BANKS:
+                if h and h[-1][0] != i and ops[h[-1][0]]["eng"] != o["eng"]:
+                    del h[:]
+            elif w and a[3] == 1:
+                h[:] = [x for x in h if not (a[1] <= x[1] and x[2] <= a[2])]
+            h.append((i, a[1], a[2], w))
+        o["deps"] = deps
+    n = len(ops)
+    users = [[] for _ in range(n)]
+    left = [len(o["deps"]) for o in ops]
+    for i, o in enumerate(ops):
+        for j in o["deps"]:
+            users[j].append(i)
+    below = [0.0] * n
+    for i in range(n - 1, -1, -1):
+        below[i] = ops[i]["cost"] + ops[i]["lat"] + LAT + max([below[u] for u in users[i]] + [0.0])
+    key = [ops[i]["prio"] * PAR["w"] - below[i] + 500.0 * NUDGE.get(i, 0) for i in range(n)]
+    ready = {e: [] for e in "VSPGY"}
+    rt = [0.0] * n
+    for i in range(n):
+        if left[i] == 0:
+            ready[ops[i]["eng"]].append(i)
+    free = {e: 0.0 for e in "VSPGY"}
+    order = {e: [] for e in "VSPGY"}
+    end = 0.0
+    for _ in range(n):
+        best = None
+        for e in "VSPGY":
+            if not ready[e]:
+                continue
+            t0 = max(free[e], min(rt[i] for i in ready[e]))
+            i = min((i for i in ready[e] if rt[i] <= t0 + PAR["look"]), key=lambda i: (key[i], i))
+            t0 = max(t0, rt[i])
+            if best is None or t0 < best[0]:
+                best = (t0, e, i)
+        t0, e, i = best
+        ready[e].remove(i)
+        order[e].append(i)
+        o = ops[i]
+        o["t0"] = t0
+        free[e] = t0 + o["cost"]
+        done = free[e] + o["lat"]
+        end = max(end, done)
+        for u in users[i]:
+            same = ops[u]["eng"] == e and o["kind"] == "c" and i not in ops[u]["hard"]
+            rt[u] = max(rt[u], free[e] if same else done + LAT)
+            left[u] -= 1
+            if left[u] == 0:
+                ready[ops[u]["eng"]].append(u)
+    return order, end
+
+
+PLAN = {}
+
+
+def rank_program(g, core, T, topo):
+    rank = T.rank_of(core)
+    if rank is None:
+        return
+    if not PLAN:
+        PLAN["ops"] = build()
+        PLAN["order"], PLAN["end"] = schedule(PLAN["ops"])
+    ops, order = PLAN["ops"], PLAN["order"]
+    cores = T.cores
+    n = len(cores)
+    queue = {"V": g.vector, "S": g.scalar, "P": g.tensor, "G": g, "Y": g.sync}
+    count = {}
+    total = {}
+    for e in "VSPG":
+        k = 0
+        for i in order[e]:
+            if ops[i]["kind"] == "c":
+                k += 1
+                count[i] = k
+        total["e" + e] = k
+    for i, o in enumerate(ops):
+        if o["kind"] == "dma":
+            total["d_" + o["name"]] = 16
+        elif o["kind"] == "send":
+            hop = o["fn"][2]
+            total["l_" + o["name"]] = len(topo.engines(core, cores[(rank + hop) % n]))
+            total["r_" + o["name"]] = len(topo.engines(cores[(rank - hop) % n], core))
+    for e in "YSPVG":
+        q = queue[e]
+        seen = {}
+        for i in order[e]:
+            o = ops[i]
+            need = {}
+            for j, raw in o["deps"].items():
+                p = ops[j]
+                if p["kind"] == "c":
+                    if p["eng"] == e and o["kind"] == "c" and j not in o["hard"]:
+                        continue
+                    s, v = "e" + p["eng"], count[j]
+                elif p["kind"] == "dma":
+                    s, v = "d_" + p["name"], 16
+                else:
+                    s = ("r_" if raw else "l_") + p["name"]
+                    v = total[s]
+                need[s] = max(need.get(s, 0), v)
+            for s, v in need.items():
+                if seen.get(s, 0) < v:
+                    q.wait_ge(T.sem[s], v)
+                    seen[s] = v
+            if o["kind"] == "c":
+                o["fn"](g, T).then_inc(T.sem["e" + e], 1)
+            elif o["kind"] == "dma":
+                o["fn"](g, T).then_inc(T.sem["d_" + o["name"]], 16)
+            else:
+                src, dst, hop = o["fn"]
+                peer = cores[(rank + hop) % n]
+                rid, pid = topo.addr(peer, core)
+                g.remote_dma(ap(T, dst), ap(T, src), T.sem["r_" + o["name"]], T.sem["l_" + o["name"]], pid, rid, topo.mask(core, peer))
+        if e == "G":
+            for s, v in total.items():
+                if seen.get(s, 0) < v:
+                    g.wait_ge(T.sem[s], v)

@@ -2,54 +2,53 @@ from concourse.bass import DstId, RemoteDMATransfer
 from concourse.mybir import dt, AluOpType as ALU, AxisListType, ActivationFunctionType as ACT
 
 BF, F32, F16, I32, U16 = "bfloat16", "float32", "float16", "int32", "uint16"
+NROT = 4
 SB = {
-    "raw": (2560, BF), "t0": (2560, F32), "t1": (2048, F32), "t2": (2048, F32), "t3": (2048, F32),
+    "raw": (2048, BF), "t0": (2048, F32), "t1": (2048, F32), "t2": (2048, F32), "t3": (2048, F32),
+    "raw2": (2048, BF), "u0": (2560, F32), "u1": (2048, F32), "u2": (2048, F32), "u3": (2048, F32), "back": (2560, BF), "w1": (1024, BF),
     "e": (4096, F16), "rr": (4096, BF), "sg": (2048, BF),
-    "ain0": (512, BF), "ain1": (512, BF), "a2e": (2048, BF), "ya": (512, BF),
-    "bg0": (1024, BF), "bg1": (1536, BF), "bgin0": (1024, BF), "bgin1": (1024, BF), "gw": (1024, F32),
-    "don0": (512, F32), "don1": (512, BF), "donin0": (512, F32), "donin1": (512, BF),
-    "cnt0": (64, BF), "cnt1": (64, BF), "cntin0": (64, BF), "cntin1": (64, BF),
-    "zao": (1024, BF), "zaj": (1024, BF), "zb": (512, BF), "m2": (512, BF), "zab": (512, BF),
-    "xb": (1536, BF), "yy": (1536, BF), "c2": (1536, BF), "ab": (4608, F32), "nk": (128, BF), "pk": (128, BF), "k8": (128, BF),
-    "cw": (32, F32), "nt": (64, F32), "q5": (384, F32),
-    "fl": (512, BF), "ob": (256, BF),
-    "hwi": (1, I32), "gli": (1, I32), "mx": (16, BF), "wf": (4, F32), "wi": (2, I32),
+    "ain0": (512, BF), "ain1": (512, BF), "a2e": (1024, BF), "ya": (512, BF), "na": (1024, BF),
+    "bg0": (1024, BF), "bg1": (1024, BF), "bgin0": (1024, BF), "bgin1": (1024, BF), "gw": (1024, F32),
+    "don0": (512, F32), "don1": (512, BF), "donin": (512, BF),
+    "ls0": (64, F16), "ls1": (64, F16), "lsin0": (96, F16), "lsin1": (96, F16),
+    "zaj": (1024, BF), "zb": (512, BF), "zab": (512, BF), "of": (512, BF), "ll": (1536, F16),
+    "yv": (512 * NROT, F16), "mk": (1536 * NROT, F16), "ab": (1536 * NROT, F32),
+    "nk": (128, BF), "pk": (128, BF), "p5": (128, BF), "n7": (128, BF),
+    "cw": (32, F32), "nt": (64, F32), "fa": (256, F32), "pick": (256, BF), "zz": (128, F32),
+    "hwi": (1, I32), "gli": (1, I32), "mx": (16, BF), "wf0": (4, F32), "wf1": (4, F32), "wi": (2, I32),
     "one": (128, BF), "idn": (128, BF), "nid": (128, BF), "blk": (128, BF), "upp": (128, BF), "b8": (8, F32), "b8a": (8, F32),
-    "qq": (128, BF), "nq": (128, BF), "wp": (144, BF), "sp": (144, BF), "fp": (144, BF), "w8": (16, BF),
-    "sm": (48, F32), "cm": (128, BF), "xp": (2, I32),
-    "x16": (16, I32), "x15": (16, I32), "x3": (8, I32), "e16": (16, F32), "e4": (4, F32), "pc": (4, F32),
+    "mat0": (288, BF), "mat1": (288, BF), "sp": (144, BF),
+    "sm": (48, F32), "cm": (128, BF), "av": (256, BF),
+    "x16": (16, I32), "x15": (16, I32), "e16": (16, F32), "pc": (4, F32),
     "ct": (1280, F32),
-    "ch": (512, BF), "dum": (64, F32), "du0": (64, F32), "base": (64, F32), "la0": (32, F32), "dif": (128, F32), "thr": (128, F32),
-    "q4": (384, F32), "ss": (384, F32), "sq": (576, F32), "ni": (576, I32), "hi": (576, I32), "off": (576, U16),
-    "boff": (64, U16), "soff": (64, U16), "uoff": (64, U16),
+    "ch": (512, F32), "dum": (64, F32), "du0": (64, F32), "base": (64, F32), "la0": (32, F32),
+    "q4": (384, F32), "ss": (384, F32), "sq": (64, F32), "sh": (32, F16), "ni": (576, I32), "hi": (576, I32), "off": (576, U16),
+    "boff": (64, U16), "boin": (32, U16), "soff": (64, U16), "uo0": (64, U16), "uo1": (64, U16), "uoin": (64, U16),
     "bv": (64, F16), "bm": (1024, F16), "eq": (1536, BF), "sf": (64, F32), "nd": (64, F32), "pi": (64, I32), "pj": (64, I32),
-    "tp": (64, F32), "ff": (32, F32), "ft0": (1056, BF), "ft1": (1056, BF), "fg": (512, BF), "ac": (64, F32), "ad": (64, F32), "ae": (64, F32),
+    "tp": (64, F32), "ff": (32, F32), "ft0": (1056, F32), "ft1": (1056, F32), "fg": (512, BF),
 }
-BANKS = ["h0", "h1", "p0", "p1", "u0", "u1", "u2", "dd"]
-SCRATCH = {k: ("sbuf", [128, v[0]], v[1]) for k, v in SB.items()}
-SZ = [2, 2, 2, 2]
-
-
-def chunks(sz):
-    SZ[:] = sz
-    for c, n in enumerate(sz):
-        SB["hz%d" % c] = (144, F16)
-        SCRATCH["hz%d" % c] = ("sbuf", [128, 36 // n, 4 * n], F16)
-
-
-chunks(list(SZ))
+ROWS = {"ct": 32}
+NHZ = 4
+for _k in range(NHZ):
+    for _n in (2, 4) if _k % 2 == 0 else (2,):
+        SB["hz%d%d" % (_n, _k)] = (144, F16)
+        ROWS["hz%d%d" % (_n, _k)] = 4 * _n
+    SB["wb%d" % _k] = (144, BF)
+    ROWS["wb%d" % _k] = 4
+BANKS = ["pb%d" % _k for _k in range(8)]
+SCRATCH = {k: ("sbuf", [128, v[0] // ROWS[k], ROWS[k]] if k in ROWS else [128, v[0]], v[1]) for k, v in SB.items()}
 for _b in BANKS:
     SCRATCH[_b] = ("psum", [128, 512], F32)
-DMAS = ["la0", "la1", "lb", "lhw", "lgl", "lmx", "y0", "y1", "y2", "y3", "lw", "lg"]
-SENDS = ["a0", "a1", "bg0", "bg1", "don0", "don1", "cnt0", "cnt1"]
+DMAS = ["la0", "la1", "lb", "lhw", "lgl", "lmx", "y0", "y1", "y2", "y3", "lw", "t010", "t020", "t030"] + ["t1%d%d" % (_d, _k) for _d in (1, 2, 3) for _k in range(3)] + ["la%d%d" % (_t, _k) for _t in range(2) for _k in range(8)]
+RELAYED = ["tab2", "tab3", "tab0", "back1"]
+SENDS = ["a0", "a1", "mat", "wf", "tab0", "tab1", "tab2", "tab3", "bo", "ls0", "ls1", "bg0", "bg1", "ab1", "back0", "back1", "don", "uo"]
 SEMAPHORES = ["eV", "eS", "eP", "eG"] + ["d_" + k for k in DMAS] + ["r_" + k for k in SENDS] + ["l_" + k for k in SENDS]
 
-PAR = {"sig": [0, 1.24, 1.91, 3.56], "look": 100.0, "w": 300.0, "ns": [1, 1, 1, 1, 1, 1, 2, 2], "k5v": [0, 0, 0, 0], "vo": 4.13,
-       "vd": 0.3, "pa": 1.25, "ma": 3.5, "f0": 1.8, "hs": 0, "h3": 0, "o1": 0, "xs": [0, 1, 0, 1, 1, 1, 1, 1], "es": 1,
-       "pro": 4.65, "f1": 9.06}
-NUDGE = {3: -2, 12: 4, 19: 8, 21: -1, 23: -4, 31: 2, 35: 8, 48: 8, 53: 4, 59: -2, 78: 5, 81: 6, 86: -1, 87: 4, 88: 8, 89: 4, 90: 6, 91: 5, 92: -2, 93: -8, 95: 1, 114: 1, 117: 2, 119: -8, 121: 4, 127: 4, 136: -6, 147: -2, 150: -8, 154: -8, 157: -1, 162: 2, 179: -1, 195: 1, 208: -8, 214: 6, 215: 12, 216: 1, 243: -4, 250: 8, 254: 8, 268: -1, 275: -1, 279: -8, 295: -2, 302: -2, 304: 2, 305: -8, 309: -1, 331: -2, 347: 4, 350: -2, 352: -1, 363: -4, 364: -8, 369: -8, 372: 1, 377: -2, 389: -2, 403: 2, 413: -4, 437: 1, 442: -1, 456: 1, 457: -1, 458: -4, 466: 8, 472: 2, 476: 2, 495: 2, 496: 2, 500: 1, 523: -8, 527: 3, 531: 2, 539: -4, 540: -4, 564: 4, 566: 2, 567: 2, 568: 2, 571: 8, 588: 1, 594: -1, 598: 2, 602: 8, 604: -4, 610: -5, 619: 1, 638: -2, 645: 2, 646: 8, 648: -8, 660: -2, 664: -1, 667: -8, 681: -1, 689: 8, 690: 2, 695: -1, 697: -8, 704: -1, 727: 8, 731: 2, 734: 4, 738: -8, 741: 2, 742: 8, 751: -8, 768: -1, 774: 2, 777: -8, 781: 4, 782: 1, 788: 4, 793: -4, 795: -4, 798: 4, 800: -6, 802: 1, 810: 6, 814: -4, 815: -2, 820: 1, 831: 4, 839: -8, 845: 1, 847: 1, 849: 1, 853: -2, 854: 1, 857: 4, 864: 2, 866: 1, 874: -1, 886: -1, 887: 2, 891: 1, 892: 4, 903: 4, 915: 1, 922: 8, 923: 2, 924: 2, 936: -2, 980: -4, 981: 4, 983: 1, 986: -2, 993: 8, 996: -1, 997: -2, 1014: 2, 1018: 4, 1020: 8, 1022: 1, 1031: 8, 1032: -4}
+PAR = {'trains': [[0, 1], [2, 3], [4, 5], [6, 7]], 'lag': [0, 0, 0, 0, 0, 0, 0, 0], 'sig': [-0.44, 1.86, 3.48, 3.09], 'look': 102.67, 'w': 1510.93, 'cp': 0.83, 'ns': [1, 1, 1, 1, 1, 1, 1, 2], 'clamp': [1, 1, 0, 0, 0, 0, 0, 0], 'rv': [0, 0, 0, 0, 0, 0, 0, 1], 'ev': [0, 0, 0, 0, 0, 0, 0, 0], 'lv': [0, 0, 0, 0, 0, 0, 0, 0], 'zv': 0, 's0': 0.41, 'ch': -0.83, 'vo': -1.14, 'pa': -4.01, 'ma': 4.7, 'f0': 5.83, 'pro': 12.04, 'f1': 9.17, 'own': -5.1, 'tb': 0.79, 'snd': -4.98, 'ah': -2.34, 'fv': 1, 'abv': 1, 'dt': [0, 0, 1, 0, 1, 1], 'la': [0, 0, 0, 0, 0, 0, 0, 0], 'df': [0, 0, 0, 0, 0, 1, 1, 1], 'early': 0.0, 'av': [1, 1], 'fs': [1, 1], 'hs': [0, 0, 0, 0, 0]}
 MAGIC = float(3 * 2 ** 34)
-CV, CP, GA, SC, LAT = 1.0, 0.5, 1.5, 3.5, 150.0
+COST = {"cv": 0.83, "cp": 0.42, "ga": 1.35, "sc": 3.8, "lat": 220.0, "own": 200.0, "mm": 0.0, "bw": 45.0, "add": 120.0, "xS": 1.0, "fS": 0.0, "xV": 1.0, "fV": 0.0}
+PASSES = 4
+MAP = {}
 
 
 def R(name, lo=0, hi=None, st=1):
@@ -63,6 +62,9 @@ def IND(win, off):
 def n_of(a):
     if a[0] == "ind":
         return 16 * n_of(a[2])
+    if a[0] in ROWS:
+        w = ROWS[a[0]]
+        return w * len(range(a[1] // w, a[2] // w, a[3]))
     return (a[2] - a[1] + a[3] - 1) // a[3]
 
 
@@ -70,17 +72,22 @@ def two(a):
     return a[0] in SB and SB[a[0]][1] in (BF, F16, U16)
 
 
+def leased(name):
+    return name[0] == "~"
+
+
 def ap(T, a):
     if not isinstance(a, tuple):
         return a
     if a[0] == "ind":
         return ap(T, a[1]).indirect(ap(T, a[2]))
-    if a[0][:2] == "hz":
-        w = SCRATCH[a[0]][1][2]
+    if a[0] in ROWS:
+        w = ROWS[a[0]]
         return T[a[0]][:, a[1] // w:a[2] // w:a[3], :]
+    name = MAP.get(a[0], a[0])
     if a[3] == 1:
-        return T[a[0]][:, a[1]:a[2]]
-    return T[a[0]][:, a[1]:a[2]:a[3]]
+        return T[name][:, a[1]:a[2]]
+    return T[name][:, a[1]:a[2]:a[3]]
 
 
 def parts(a):
@@ -91,11 +98,27 @@ def parts(a):
     return [a]
 
 
+def waves():
+    out = []
+    for k, tr in enumerate(PAR["trains"]):
+        for w in range(20):
+            now = [(m, w - PAR["lag"][m]) for m in tr if 0 <= w - PAR["lag"][m] < 4]
+            while now:
+                n = 4 if len(now) == 4 else 2 if len(now) > 1 and now[1][0] == now[0][0] + 1 else 1
+                out.append((w + PAR["sig"][k], now[:n]))
+                now = now[n:]
+    return out
+
+
 def build():
     ops = []
     pr = [0.0]
-    sz = SZ
-    m0 = [sum(sz[:c]) for c in range(len(sz))]
+    nb = [0]
+    CV, CP, GA, SC = COST["cv"], COST["cp"], COST["ga"], COST["sc"]
+
+    def bank():
+        nb[0] += 1
+        return "~%d" % nb[0]
 
     def add(eng, fn, rd, wr, cost, kind="c", name=None, lat=0.0):
         r2 = [x for a in rd for x in parts(a)]
@@ -105,6 +128,8 @@ def build():
                 w2.append(a[1]); r2.append(a[2])
             else:
                 w2.append(a)
+        if kind == "c" and eng in "SV":
+            cost = cost * COST["x" + eng] + COST["f" + eng]
         ops.append({"eng": eng, "fn": fn, "rd": r2, "wr": w2, "cost": cost, "kind": kind, "name": name, "prio": pr[0], "lat": lat})
 
     def vcost(out, ins, base):
@@ -128,7 +153,7 @@ def build():
 
     def tt(out, a, b, op):
         add("V", lambda g, T: g.vector.tensor_tensor(ap(T, out), ap(T, a), ap(T, b), op), [a, b], [out],
-            vcost(out, [a], 1 if a[0] in BANKS or b[0] in BANKS else 2))
+            vcost(out, [a], 1 if leased(a[0]) or leased(b[0]) else 2))
 
     def ms(out, c):
         add("V", lambda g, T: g.vector.memset(ap(T, out), c), [], [out], CV * max(64, n_of(out) * (0.5 if two(out) else 1)))
@@ -144,7 +169,7 @@ def build():
                 ins = g.tensor.matmul(ap(T, o), ap(T, l), ap(T, r), start and i == 0, stop and i == len(lst) - 1)
             return ins
         c = sum(max(min(64, n_of(l)), n_of(r)) * (4 if SB[l[0]][1] == F32 else 1) for o, l, r in lst)
-        add("P", fn, [x for o, l, r in lst for x in (l, r)], [o for o, l, r in lst], CP * c)
+        add("P", fn, [x for o, l, r in lst for x in (l, r)], [o for o, l, r in lst], CP * c + COST["mm"] * len(lst))
 
     def iota(out, pat, base, cm=0):
         if SB[out[0]][1] == I32:
@@ -159,7 +184,7 @@ def build():
         def fn(g, T):
             q = g.sync if eng == "Y" else g.scalar
             return q.dma_start(ap(T, out), src(T))
-        add(eng, fn, [], [out], 100, "dma", name, 2000 + n_of(out) * 1.5)
+        add(eng, fn, [], [out], 100, "dma", name, 1800 + n_of(out) * 1.0)
 
     def store(eng, name, a, at=None):
         at = a[1] if at is None else at
@@ -167,10 +192,20 @@ def build():
         def fn(g, T):
             q = g.sync if eng == "Y" else g.scalar
             return q.dma_start(T.y[:, at:at + n_of(a)], ap(T, a))
-        add(eng, fn, [a], [], 100, "dma", name, 2000 + n_of(a) * 1.5)
+        add(eng, fn, [a], [], 100, "dma", name, 1800 + n_of(a) * 1.0)
 
     def send(name, src, dst, hop):
-        add("G", (src, dst, hop), [src], [dst], 1000, "send", name, 2500 + n_of(src) * (2 if two(src) else 4) * 128 / 40.0)
+        add("G", (src, dst, hop), [src], [dst], 800, "send", name, 1800 + n_of(src) * (2 if two(src) else 4) * 128 / COST["bw"])
+
+    def dadd(name, out, a):
+        add("G", lambda g, T: g.dma_start(ap(T, out), ap(T, a), accum_op=ALU.add), [a, out], [out], 1000, "dma", name,
+            2200 + n_of(a) * (2 if two(a) else 4) * 128 / COST["add"])
+
+    def empty(out, a):
+        if PAR["zv"]:
+            ts(out, a, 0.0, ALU.is_equal)
+        else:
+            act(out, a, ACT.Relu, bias=1.0, scale=-1.0)
 
     pr[0] = -10
     load("Y", "la0", R("raw", 0, 512), lambda T: T.ent[:, 0:512])
@@ -186,322 +221,420 @@ def build():
     sel(R("b8a"), R("one", 0, 8), [[-16, 8]], ALU.is_ge, 0, 1)
     sel(R("b8"), R("b8a"), [[16, 8]], ALU.is_ge, 15, -1)
     sel(R("idn"), R("one"), [[-1, 128]], ALU.is_equal, 0, 1)
-    for k in ("wp", "sp", "fp"):
-        ms(R(k), 0.0)
-    ms(R("cm"), -2048.0)
+    ms(R("mat0", 0, 144), 0.0)
+    ms(R("sp"), 0.0)
+    ms(R("wf0"), 0.0)
+    ms(R("cm", 0, 64), -2048.0)
+    ms(R("cm", 64, 128), 4096.0)
     ts(R("x15"), R("x16"), 15, ALU.bitwise_and)
-    ts(R("x3", 0, 4), R("x16", 0, 4), 3, ALU.bitwise_and)
     ts(R("e16"), R("x15"), 0.0, ALU.is_equal)
-    ts(R("e4"), R("x3", 0, 4), 0.0, ALU.is_equal)
     cp_(R("pc", 0, 1), R("x15", 0, 1))
     ts(R("nid"), R("idn"), -1.0, ALU.mult)
-    cp_(R("wf", 0, 1), R("hwi"))
+    cp_(R("wf0", 0, 1), R("hwi"))
     ts(R("wi", 0, 1), R("hwi"), 15, ALU.bitwise_and)
-    cp_(R("wf", 1, 2), R("wi", 0, 1))
-    ts(R("wp", 15, 143, 16), R("b8"), R("wf", 0, 1), ALU.mult)
-    ts(R("w8", 0, 8), R("b8"), R("wf", 0, 1), ALU.mult)
-    ts(R("w8", 8, 16), R("b8"), R("wf", 1, 2), ALU.mult, -256.0, ALU.mult)
-    nc = len(sz)
+    cp_(R("wf0", 1, 2), R("wi", 0, 1))
+    ts(R("mat0", 15, 143, 16), R("b8"), R("wf0", 0, 1), ALU.mult)
+    ts(R("mat0", 144, 152), R("b8"), R("wf0", 0, 1), ALU.mult)
+    ts(R("mat0", 152, 160), R("b8"), R("wf0", 1, 2), ALU.mult, -256.0, ALU.mult)
     for m in range(8):
-        act(R("ct", 32 * m, 32 * m + 32), R("one", 0, 32), ACT.Identity, scale=-256.0 * (2 * m + 1) ** 2)
+        ms(R("ct", 160 * m, 160 * m + 32), -256.0 * (2 * m + 1) ** 2)
     for d in range(1, 5):
-        act(R("ct", 256 * d, 256 * d + 256), R("ct", 0, 256), ACT.Identity, bias=32.0 * 811 * d)
-    for a in range(8):
-        act(R("blk", 16 * a, 16 * a + 16), R("one", 0, 16), ACT.Identity, scale=R("b8", a, a + 1))
+        act(R("ct", 32 * d, 1280, 5), R("ct", 0, 1280, 5), ACT.Identity, bias=32.0 * 811 * d)
+    iota(R("av"), [[32, 8], [0, 32]], 2064)
+    sel(R("upp"), R("one"), [[-16, 8], [0, 16]], ALU.is_ge, 0, 1)
+    sel(R("blk"), R("upp"), [[16, 8], [0, 16]], ALU.is_ge, 15, -1)
     pr[0] = -8
-    tb = ["p0", "p1", "u0", "u1"]
     for k in (0, 2, 3, 1):
-        lo = 512 * k
+        lo, b = 512 * k, bank()
         ts(R("sg", lo, lo + 512), R("raw", lo, lo + 512), 0.0, ALU.is_gt, 2048.0, ALU.mult)
-        mm([(R(tb[k]), R("idn"), R("raw", lo, lo + 512)), (R(tb[k]), R("idn"), R("sg", lo, lo + 512))])
-        act(R("t0", lo, lo + 512), R(tb[k]), ACT.Identity, bias=-1024.0)
+        mm([(R(b), R("idn"), R("raw", lo, lo + 512)), (R(b), R("idn"), R("sg", lo, lo + 512))])
+        act(R("t0", lo, lo + 512), R(b), ACT.Identity, bias=-1024.0)
     pr[0] = -7
-    send("a1", R("raw", 512, 1024), R("ain1"), 2)
-    for c in range(nc):
-        if sz[c] < 4:
-            ts(R("hz%d" % c, 0, 144), R("wp", 0, 144), 0.0, ALU.mult)
+    for name in sorted(set("hz%d%d" % (len(w[1]), w[1][0][0] // 2) for w in waves() if len(w[1]) < 4)) + ["wb%d" % k for k in range(NHZ)]:
+        ts(R(name), R("mat0", 0, 144), 0.0, ALU.mult)
     sel(R("upp"), R("blk"), [[1, 128]], ALU.is_gt, 0, -1)
     iota(R("du0"), [[0, 32], [16, 2]], 1025)
     iota(R("la0"), [[16, 32]], 0)
-    iota(R("ch"), [[1, 16], [0, 32]], 0)
+    iota(R("ch"), [[1, 16], [0, 32]], 20)
     iota(R("ft0"), [[0, 1056]], 0)
 
-    def index_chain(bank, o, beta, w=64):
-        if PAR["o1"]:
-            act(R("q5", o, o + w), R(bank, 0, w), ACT.Identity, bias=MAGIC)
-            act(R("q4", o, o + w), R("q5", o, o + w), ACT.Identity, bias=-MAGIC)
-        else:
-            ts(R("q4", o, o + w), R(bank, 0, w), MAGIC, ALU.add, MAGIC, ALU.subtract)
-        tt(R("ss", o, o + w), R(bank, 0, w), R("q4", o, o + w), ALU.subtract)
-        act(R("sq", o, o + w), R("ss", o, o + w), ACT.Square, bias=beta)
-
     pr[0] = -6
-    mm([(R("h1", 0, 64), R("idn"), R("cm", 0, 64))] + [(R("h1", 0, 64), R("wp", 15 - r, 143 - r), R("raw", r, 1024, 16)) for r in range(16)])
-    index_chain("h1", 256, 2048.0 + 592)
-    ts(R("ni", 256, 320), R("sq", 256, 320), -592.0 * 592, ALU.add)
+    b = bank()
+    mm([(R(b, 0, 64), R("idn"), R("cm", 0, 64))] + [(R(b, 0, 64), R("mat0", 15 - r, 143 - r), R("raw", r, 1024, 16)) for r in range(16)])
+    ts(R("q4", 256, 320), R(b, 0, 64), MAGIC, ALU.add, MAGIC, ALU.subtract)
+    tt(R("ss", 256, 320), R(b, 0, 64), R("q4", 256, 320), ALU.subtract)
+    act(R("sq"), R("ss", 256, 320), ACT.Square, bias=2048.0 + 592)
+    ts(R("ni", 256, 320), R("sq"), -592.0 * 592, ALU.add)
     ts(R("hi", 256, 320), R("ni", 256, 320), 5, ALU.arith_shift_right, 1023, ALU.bitwise_and)
     cp_(R("boff"), R("hi", 256, 320))
     ts(R("bv"), R("hi", 256, 320), 1.0, ALU.add)
-    pr[0] = 2.0
+    pr[0] = PAR["own"]
     for r in range(16):
         ts(R("bm", 64 * r, 64 * r + 64), R("bv"), R("e16", r, r + 1), ALU.mult)
-    for k, b in enumerate(("u2", "dd")):
+    for k in range(2):
+        b = bank()
         mm([(R(b), R("upp"), R("bm", 512 * k, 512 * k + 512))] + [(R(b, 64 * r, 64 * r + 64), R("nid"), R("bv")) for r in range(8)])
         ts(R("eq", 512 * k, 512 * k + 512), R(b), 0.0, ALU.is_equal, 2048.0, ALU.mult)
-    mm([(R("u2"), R("blk"), R("bm", 0, 1024, 2))] + [(R("u2", 32 * r, 32 * r + 32), R("nid"), R("bv", 1, 64, 2)) for r in range(16)])
-    ts(R("eq", 1024, 1536), R("u2"), 0.0, ALU.is_equal, 2048.0, ALU.mult)
-    mm([(R("dd", 0, 64), R("idn"), R("bv"))] + [(R("dd", 0, 64), R("idn"), R("eq", 64 * r, 64 * r + 64)) for r in range(16)]
-       + [(R("dd", 1, 64, 2), R("idn"), R("eq", 1024 + 32 * r, 1056 + 32 * r)) for r in range(16)])
+    b = bank()
+    mm([(R(b), R("blk"), R("bm", 0, 1024, 2))] + [(R(b, 32 * r, 32 * r + 32), R("nid"), R("bv", 1, 64, 2)) for r in range(16)])
+    ts(R("eq", 1024, 1536), R(b), 0.0, ALU.is_equal, 2048.0, ALU.mult)
+    b = bank()
+    mm([(R(b, 0, 64), R("idn"), R("bv"))] + [(R(b, 0, 64), R("idn"), R("eq", 64 * r, 64 * r + 64)) for r in range(16)]
+       + [(R(b, 1, 64, 2), R("idn"), R("eq", 1024 + 32 * r, 1056 + 32 * r)) for r in range(16)])
     ts(R("dum"), R("du0"), R("pc", 0, 1), ALU.add)
-    tt(R("sf"), R("dd", 0, 64), R("dum"), ALU.min)
+    tt(R("sf"), R(b, 0, 64), R("dum"), ALU.min)
     ts(R("soff"), R("sf"), -1.0, ALU.add)
     ts(R("nd"), R("sf"), 1024.5, ALU.is_lt)
     ts(R("pi"), R("ss", 256, 320), 2048.0, ALU.add)
     ts(R("pj"), R("pi"), 1, ALU.bitwise_and)
-    ts(R("tp"), R("pj"), 5.5, ALU.add)
+    ts(R("tp"), R("pj"), 6.5, ALU.add, -4096.0, ALU.mult)
     tt(R("nt"), R("tp"), R("nd"), ALU.mult)
     ts(R("base", 0, 32), R("la0"), R("pc", 0, 1), ALU.add, 1024.0, ALU.add)
     ts(R("base", 32, 64), R("base", 0, 32), -512.0, ALU.add)
     for t in range(2):
-        tt(R("dif", 64 * t, 64 * t + 32), R("hi", 256 + 32 * t, 288 + 32 * t), R("base", 0, 32), ALU.subtract)
-        ms(R("dif", 64 * t + 32, 64 * t + 64), -512.0)
+        cp_(R("ls%d" % t, 32, 64), R("hi", 256 + 32 * t, 288 + 32 * t))
+        ts(R("lsin%d" % t, 64, 96), R("la0"), R("pc", 0, 1), ALU.add)
     cp_(R("sp", 15, 143, 16), R("b8"))
-    pr[0] = 3.0
+    pr[0] = -4.0
     iota(R("ft1"), [[0, 1056]], 0)
-    iota(R("t0", 2048, 2560), [[0, 512]], 0)
-    iota(R("raw", 2048, 2560), [[0, 512]], 0)
-    add("Y", lambda g, T: g.sync.dma_start(T.gw[:, 512:1024], T.t0[:, 0:512]), [R("t0", 0, 512)], [R("gw", 512, 1024)], 100, "dma", "lg", 3500)
-    load("Y", "lw", R("bg1", 1024, 1536), lambda T: T.ent[:, 512:1024])
+    load("Y", "lw", R("w1", 512, 1024), lambda T: T.ent[:, 512:1024])
     for a in range(8):
-        act(R("qq", 16 * a, 16 * a + 16), R("mx"), ACT.Identity, scale=R("b8", a, a + 1))
-    act(R("nk"), R("idn"), ACT.Identity, scale=-256.0)
-    act(R("pk"), R("idn"), ACT.Identity, scale=256.0)
-    act(R("k8"), R("idn"), ACT.Identity, scale=2048.0)
-    iota(R("cw"), [[16, 16], [0, 2]], 0)
-    ts(R("wf", 2, 3), R("gli"), -1.0, ALU.mult)
+        act(R("mat0", 160 + 16 * a, 176 + 16 * a), R("mx"), ACT.Identity, scale=R("b8", a, a + 1))
+    for k, s in (("nk", -256.0), ("pk", 256.0), ("p5", 512.0), ("n7", -768.0)):
+        ts(R(k), R("idn"), s, ALU.mult)
+    ms(R("pick"), 4096.0)
+    sel(R("pick"), R("pick"), [[-1, 4], [0, 2], [-4, 32]], ALU.is_equal, 0, 1)
+    iota(R("cw"), [[16, 16], [0, 2]], 320)
+    ts(R("wf0", 2, 3), R("gli"), -1.0, ALU.mult)
     ms(R("sm"), 0.0)
-    for lo, s in ((0, 1.0), (8, 1.0), (16, -1.0), (40, -1.0)):
+    for lo, s in ((0, -1.0), (8, 1.0), (16, 1.0), (40, -1.0)):
         ts(R("sm", lo, lo + 8), R("b8"), s, ALU.mult)
-    for b in range(4):
-        ts(R("fp", 12 + b, 140 + b, 16), R("b8"), R("e4", b, b + 1), ALU.mult)
+    pr[0] = PAR["snd"]
+    send("a1", R("raw", 512, 1024), R("ain1"), -1)
+    send("mat", R("mat0"), R("mat1"), 1)
+    send("wf", R("wf0"), R("wf1"), 1)
+    send("bo", R("boff", 32, 64), R("boin"), 1)
+    for k, name in enumerate(["t1", "t2", "t3", "u1", "u2", "u3"]):
+        pr[0] = PAR["snd"] + 2 * (k // 3)
+        for lo in range(0, 2048 * PAR["dt"][k], 512):
+            iota(R(name, lo, lo + 512), [[0, 512]], -256 * (k % 3 + 1))
+    iota(R("u0", 2048, 2560), [[0, 512]], 0)
+    iota(R("back", 2048, 2560), [[0, 512]], 0)
 
-    def first_lanes(t, bank):
-        ft = "ft%d" % t
+    def first_lanes(t):
+        ft, b = "ft%d" % t, bank()
         for k in range(15, -1, -1):
-            cp_(IND(R(ft), R("soff", 32 * t + 2 * k, 32 * t + 2 * k + 2)), R("ch", 32 * k, 32 * k + 32))
+            out, a = IND(R(ft), R("soff", 32 * t + 2 * k, 32 * t + 2 * k + 2)), R("ch", 32 * k, 32 * k + 32)
+            if PAR["fs"][t]:
+                add("S", lambda g, T, out=out, a=a: g.scalar.activation(ap(T, out), ap(T, a), ACT.Silu), [a], [out], 65 + CV * SC * 32)
+            else:
+                cp_(out, a)
         act(R("fg"), IND(R(ft), R("boff", 32 * t, 32 * t + 32)), ACT.Copy)
-        mm([(R(bank, 0, 32), R("sp", 15 - r, 143 - r), R("fg", r, 512, 16)) for r in range(16)])
-        tt(R("ff"), R(bank, 0, 32), R("cw"), ALU.is_equal)
-        for k in range(2):
-            tt(R("thr", 64 * t + 32 * k, 64 * t + 32 * k + 32), R("ff"), R("nt", 32 * t, 32 * t + 32), ALU.mult)
+        mm([(R(b, 0, 32), R("sp", 15 - r, 143 - r), R("fg", r, 512, 16)) for r in range(16)])
+        tt(R("ff"), R(b, 0, 32), R("cw"), ALU.is_equal)
+        tt(R("ls%d" % t, 0, 32), R("ff"), R("nt", 32 * t, 32 * t + 32), ALU.mult)
+        send("ls%d" % t, R("ls%d" % t), R("lsin%d" % t, 0, 64), 1 - 2 * t)
 
-    pr[0] = PAR["f0"]
-    first_lanes(0, "dd")
-    tabs = ["t0", "t1", "t2", "t3", "raw"]
-
-    def to_offsets(bank, d, col, o, w):
-        tt(R("ni", o, o + w), R(bank, 256, 256 + w), R("ct", 256 * d + col, 256 * d + col + w), ALU.add)
+    def to_offsets(sq, ct, o):
+        w = n_of(sq)
+        tt(R("ni", o, o + w), sq, ct, ALU.add)
         ts(R("hi", o, o + w), R("ni", o, o + w), 5, ALU.arith_shift_right, 2047, ALU.bitwise_and)
         cp_(R("off", o, o + w), R("hi", o, o + w))
 
     def prologue(t):
-        ain, o = "ain%d" % t, 320 * t
-        mm([(R("h0", 0, 32), R("idn"), R("cm", 0, 32))] + [(R("h0", 0, 32), R("wp", 15 - r, 143 - r), R(ain, r, 512, 16)) for r in range(16)])
-        ts(R("q4", o, o + 32), R("h0", 0, 32), MAGIC, ALU.add, MAGIC, ALU.subtract)
-        tt(R("ss", o, o + 32), R("h0", 0, 32), R("q4", o, o + 32), ALU.subtract)
-        act(R("a2e", 512 * t, 512 * t + 512), R(ain), ACT.Identity, bias=-256.0)
-        for c in range(2):
-            for k in range(4):
-                act(R("h%d" % c, 256 + 32 * k, 288 + 32 * k), R("ss", o, o + 32), ACT.Square, bias=2064.0 + 32 * (4 * c + k))
-            to_offsets("h%d" % c, 0, 128 * c, o + 128 * c, 128)
-        act(R("zao", 512 * t, 512 * t + 512), R("raw", 512 * t, 512 * t + 512), ACT.Relu, bias=1.0, scale=-1.0)
-        act(R("zaj", 512 * t, 512 * t + 512), R(ain), ACT.Relu, bias=1.0, scale=-1.0)
+        ain, o, b = "ain%d" % t, 320 * t, bank()
+        mm([(R(b, 0, 32), R("idn"), R("cm", 0, 32))] + [(R(b, 0, 32), R("mat%d" % t, 15 - r, 143 - r), R(ain, r, 512, 16)) for r in range(16)])
+        ts(R("q4", o, o + 32), R(b, 0, 32), MAGIC, ALU.add, MAGIC, ALU.subtract)
+        ss = R("sh") if t else R("ss", o, o + 32)
+        tt(ss, R(b, 0, 32), R("q4", o, o + 32), ALU.subtract)
+        if PAR["av"][t]:
+            ts(R("a2e", 512 * t, 512 * t + 512), R(ain), -256.0, ALU.add)
+        else:
+            act(R("a2e", 512 * t, 512 * t + 512), R(ain), ACT.Identity, bias=-256.0)
+        for ms_ in ([[0, 1], [2, 3], [4, 5, 6, 7]] if t == 0 else [list(range(8))]):
+            b = bank()
+            if t:
+                mm([(R(b, 256, 512), R("idn"), R("av"))] + [(R(b, 256 + 32 * m, 288 + 32 * m), R("idn"), ss) for m in ms_])
+                act(R(b, 0, 256), R(b, 256, 512), ACT.Square)
+            for k, m in enumerate(ms_ * (1 - t)):
+                act(R(b, 32 * k, 32 * k + 32), ss, ACT.Square, bias=2064.0 + 32 * m)
+            to_offsets(R(b, 0, 32 * len(ms_)), R("ct", 160 * ms_[0], 160 * ms_[-1] + 32, 5), o + 32 * ms_[0])
+        empty(R("zaj", 512 * t, 512 * t + 512), R(ain))
 
+    wv = waves()
+    pos = {}
+    for k, tr in enumerate(PAR["trains"]):
+        for m in tr:
+            pos[m] = PAR["lag"][m] + PAR["sig"][k]
+    done_order = sorted(range(8), key=lambda m: (pos[m], m))
     nblk = [0]
-    nu = [0]
+    nhz = [0]
     for t in range(2):
         P0 = 100.0 * t
         ain, bg, bgin = "ain%d" % t, "bg%d" % t, "bgin%d" % t
-        zao, zaj = R("zao", 512 * t, 512 * t + 512), R("zaj", 512 * t, 512 * t + 512)
-        bo = R("boff", 32 * t, 32 * t + 32)
+        zaj = R("zaj", 512 * t, 512 * t + 512)
+        bo = R("boin") if t else R("boff", 0, 32)
+        tabs = [["t0", "t1", "t2", "t3", "raw"], ["u0", "u1", "u2", "u3", "raw2"]]
+        mat, qq, aim = "mat%d" % t, R("mat%d" % t, 160, 288), R("wf%d" % t, 2, 3)
         if t == 0:
-            pr[0] = -5
+            pr[0] = -8.5
             prologue(0)
         else:
             pr[0] = 40
-            tt(R("ac"), R("cntin0"), R("thr", 0, 64), ALU.is_lt)
-            tt(R("ad"), R("ac"), R("dif", 0, 64), ALU.mult)
-            tt(R("ae"), R("ad"), R("base"), ALU.add)
-            cp_(R("uoff"), R("ae"))
-            cp_(IND(R("t0", 1024, 2560), R("uoff", 0, 32)), R("donin0"))
-            act(R("t0", 0, 512), IND(R("gw"), R("uoff", 32, 64)), ACT.Copy)
-        spans = [(0, 2048)] if t == 0 else [(1024, 2048), (0, 512)]
+            cp_(IND(R("u0", 1024, 2560), R("uo0", 0, 32)), R("don0"))
+            act(R("u0", 0, 512), IND(R("gw"), R("uo0", 32, 64)), ACT.Copy)
+        spans = [(0, 1024), (1024, 2048)] if t == 0 else [(0, 512), (1024, 1536), (1536, 2048)]
         ev = []
-        left = [2048, 2048]
+        cb = bank()
+        dd = {}
+        nd = [0]
 
-        def tables(d):
+        def tables(d, t=t, spans=spans):
+            if d < 4 and PAR["dt"][3 * t + d - 1]:
+                for lo, hi in [(0, 2048)] if t == 0 else spans if len(spans) == 1 else [(0, 512), (1024, 2048)]:
+                    dadd("t%d%d%d" % (t, d, lo // 512), R(tabs[t][d], lo, hi), R(tabs[t][0], lo, hi))
+                return
             for lo, hi in spans:
                 if d < 4:
-                    act(R(tabs[d], lo, hi), R("t0", lo, hi), ACT.Identity, bias=-256.0 * d)
+                    act(R(tabs[t][d], lo, hi), R(tabs[t][0], lo, hi), ACT.Identity, bias=-256.0 * d)
                 else:
-                    act(R("raw", lo, hi), R("t0", lo, hi), ACT.Relu, bias=-1024.0)
+                    act(R(tabs[t][4], lo, hi), R(tabs[t][0], lo, hi), ACT.Relu, bias=-1024.0)
+
+        def ahead():
+            for d in range(1, 5):
+                tables(d, 1, [(512, 1024)])
+            b = bank()
+            ts(R("ya"), R(bgin, 512, 1024), 0.0, ALU.is_gt, 2048.0, ALU.mult)
+            mm([(R(b), R("idn"), R(bgin, 512, 1024)), (R(b), R("idn"), R("ya"))])
+            act(R("gw", 0, 512), R(b), ACT.Identity, bias=-1024.0)
 
         def partners():
-            act(R(bg, 0, 512), IND(R("raw", 1024, 2048), bo), ACT.Copy)
-            mm([(R("p0"), R("idn"), R(bg, 0, 512)), (R("p0"), R("pk"), zao)])
-            act(R("ya"), R("p0"), ACT.Relu, bias=-256.0)
-            mm([(R("p1"), R("idn"), R("raw", 512 * t, 512 * t + 512)), (R("p1"), R("idn"), R("ya"))])
-            act(R(bg, 512, 1024), R("p1"), ACT.Identity)
-            send(bg, R(bg, 0, 1024), R(bgin), 1 + t)
+            A, at = (R("raw2", 512, 1024), bg) if t else (R(ain), bgin)
+            act(R(bg, 0, 512), IND(R(tabs[t][4], 1024, 2048), bo), ACT.Copy)
             if t == 0:
-                act(R("ya"), R(bg, 512, 1024), ACT.Sign)
-                mm([(R("p1"), R("idn"), R(bg, 512, 1024)), (R("p1"), R("k8"), R("ya"))])
-                act(R("gw", 0, 512), R("p1"), ACT.Identity, bias=-1024.0)
+                send(bg, R(bg, 0, 512), R(bgin, 0, 512), 1)
+            b, na = bank(), R("na", 512 * t, 512 * t + 512)
+            if PAR["abv"]:
+                ts(na, A, 0.0, ALU.is_gt, -256.0, ALU.mult)
+                mm([(R(b), R("idn"), R(at, 0, 512)), (R(b), R("idn"), na)])
+                tt(R(at, 512, 1024), R(b), A, ALU.max)
+            else:
+                act(na, A, ACT.Sign)
+                mm([(R(b), R("idn"), R(at, 0, 512)), (R(b), R("nk"), na)])
+                act(na, R(b), ACT.Relu)
+                b = bank()
+                mm([(R(b), R("idn"), A), (R(b), R("idn"), na)])
+                act(R(at, 512, 1024), R(b), ACT.Identity)
+            if t == 1:
+                send(bg, R(bg, 0, 1024), R(bgin), 2)
+            if t == 0:
+                for k in range(4):
+                    send("tab%d" % k, R("t0", 512 * k, 512 * k + 512), R("u0", 512 * k, 512 * k + 512) if k else R("gw", 512, 1024), 1)
+                    if "tab%d" % k not in RELAYED:
+                        ops[-1]["after"] = ["bg0"]
+            else:
+                pr[0] += 3
+                send("ab1", R(bg, 512, 1024), R("w1", 0, 512), -1)
+                send("back0", R("raw2", 0, 512), R("back", 0, 512), -1)
+                ops[-1]["after"] = ["bg1"]
+                send("back1", R("raw2", 1024, 2048), R("back", 1024, 2048), -1)
+                ops[-1]["after"] = ["bg1"]
+                store("Y", "y0", R("back", 0, 512))
 
         def masks():
-            act(R("zb"), R(bgin, 0, 512), ACT.Relu, bias=1.0, scale=-1.0)
-            act(R("zab"), R(bgin, 512, 1024), ACT.Relu, bias=1.0, scale=-1.0)
-
-        def step(c, d):
-            n, o = sz[c], 32 * m0[c]
-            lo, hi = 512 * m0[c], 512 * (m0[c] + n)
-            rr = R("rr", lo, hi)
-            if d == 4 and c == 0:
-                act(R("don%d" % t), IND(R("t0" if t == 0 else "raw", 0, 2048), R("off", 0, 32)), ACT.Copy)
-                send("don%d" % t, R("don%d" % t), R("donin%d" % t), -1 - t)
-            w = 256 if PAR["hs"] else 512
-            oo = o + (320 * t if d == 0 else 0)
-            for k in range(512 * n // w):
-                ek = R("e", lo + w * k, lo + w * k + w)
-                al = 512 * t + w * k % 512
-                tt(ek, IND(R(tabs[d], 0, 2048), R("off", oo + w * k // 16, oo + (w * k + w) // 16)), R("a2e", al, al + w) if d == 0 else ek, ALU.max)
-                if d < 4 and (w * k + w) % 512 == 0:
-                    act(R("rr", ek[2] - 512, ek[2]), R("e", ek[2] - 512, ek[2]), ACT.Identity, bias=144.0 - 127.5 / 256, scale=1.0 / 256)
-            if d == 4:
+            zb, zab = R("zb"), R("zab")
+            empty(zb, R(bgin, 0, 512))
+            empty(zab, R(bgin, 512, 1024))
+            if not any(PAR["clamp"]):
                 return
-            bank, st, w = ["h0", "h1", "u2"][c % (2 + PAR["h3"])], 4 * n, 32 * n
-            me = [(R(bank, 0, w), R("idn"), R("cm", 0, w))] + [(R(bank, r, w, st), R("e", lo + r, hi, st), R("w8", 0, 8)) for r in range(st)]
-            mr = [(R(bank, r, w, st), R("rr", lo + r, hi, st), R("w8", 8, 16)) for r in range(st)]
-            if PAR["es"]:
-                mm(me, stop=False)
-                mm(mr, start=False)
-            else:
-                mm(me + mr)
-            hz, rep = "hz%d" % c, 4 // n
-            ts(R("q4", o, o + w), R(bank, 0, w), MAGIC, ALU.add, MAGIC, ALU.subtract)
-            tt(R(hz, 16 - st, 144 - st, rep), R(bank, 0, w), R("q4", o, o + w), ALU.subtract)
-            mm([(R(bank, 128, 128 + w), R(hz, 16 - st - st * k, 144 - st - st * k), R("idn", k, 128, rep)) for k in range(rep)])
-            for k in range(n):
-                act(R(bank, 256 + 32 * k, 288 + 32 * k), R(bank, 128 + 32 * k, 160 + 32 * k), ACT.Square, bias=2064.0 + 32 * (m0[c] + k))
-            to_offsets(bank, d + 1, o, o, w)
-            if d == 3:
-                if PAR["k5v"][c]:
-                    ts(rr, rr, -144.0, ALU.add, 0.0, ALU.max)
-                else:
-                    act(rr, rr, ACT.Relu, bias=-144.0)
+            for out, lst, c in ((R("of"), [("n7", zaj), ("nk", zb), ("p5", zab)], 768.0),
+                                (R("ll", 0, 512), [("idn", R(bgin, 0, 512)), ("p5", zaj), ("pk", zb), ("nk", zab)], -768.0),
+                                (R("ll", 512, 1024), [("idn", R(ain)), ("p5", zaj), ("nk", zab)], -512.0),
+                                (R("ll", 1024, 1536), [("idn", R(bgin, 512, 1024)), ("pk", zaj)], -512.0)):
+                b = bank()
+                mm([(R(b), R(l), r) for l, r in lst])
+                act(out, R(b), ACT.Identity, bias=c)
 
-        def verdict(c, mb, s, ns):
-            k = nblk[0]; nblk[0] += 1
-            m, w = m0[c] + mb, 512 // ns
-            pb, ub, o = R("p%d" % (k % 2), 0, w), R("u%d" % (k % 3), 0, w), 512 * (k % 3)
-            ao = 1536 * (k % 3)
-            xb, yy, c2 = R("xb", o, o + w), R("yy", o, o + w), R("c2", o, o + w)
-            mm([(pb, R("idn"), R("e", 512 * m + s, 512 * m + 512, ns)), (pb, R("nk"), R("rr", 512 * m + s, 512 * m + 512, ns))])
-            q, nq = R("qq"), R("nq")
-            lanes = [R(bgin, s, 512, ns), R(ain, s, 512, ns), R(bgin, 512 + s, 1024, ns)]
-            tt(xb, pb, R("zb", s, 512, ns), ALU.mult)
-            za = R("zaj", 512 * t + s, 512 * t + 512, ns)
-            tt(yy, pb, za, ALU.mult)
-            if PAR["xs"][m]:
-                tt(c2, pb, R("zab", s, 512, ns), ALU.mult)
-            else:
-                pb = R("u%d" % (nu[0] % (3 - PAR["h3"])), 0, w); nu[0] += 1
-                mm([(pb, R("idn"), xb), (pb, R("pk"), za)])
-                act(c2, pb, ACT.Relu, bias=-256.0)
-            for x in range(3):
-                ub = R("u%d" % (nu[0] % (3 - PAR["h3"])), 0, w); nu[0] += 1
-                mm([(ub, q, lanes[x]), (ub, q, (xb, yy, c2)[x])])
-                act(R("ab", ao + 512 * x, ao + 512 * x + w), ub, ACT.Abs, bias=R("wf", 2, 3))
-            half, ml = m // 4, m % 4
-            for b in range(4 // ns):
-                out = R("dd", 256 * half + 4 * ml + s + ns * b, 256 * half + 256, 16)
-                mm([(out, R("ab", ao + 512 * x + b, ao + 512 * x + w, 4 // ns), R("sm", 32 - 16 * x, 48 - 16 * x)) for x in range(3)])
-            left[half] -= w
-            if left[half] == 0:
-                o = 256 * half
-                if left[1 - half]:
-                    act(R("fl", o, o + 256), R("dd", o, o + 256), ACT.Relu)
+        def step(m, d):
+            lo = 512 * m
+            ek, rr = R("e", lo, lo + 512), R("rr", lo, lo + 512)
+            oo = 32 * m + (320 * t if d == 0 else 0)
+            if d == 4 and m == 0:
+                act(R("don%d" % t), IND(R("t0" if t == 0 else "raw2", 0, 2048), R("off", 0, 32)), ACT.Copy)
+                if t == 1:
+                    send("don", R("don1"), R("donin"), 1)
+            w = 256 if PAR["hs"][d] else 512
+            for c in range(0, 512, w):
+                ec = R("e", lo + c, lo + c + w)
+                tt(ec, IND(R(tabs[t][d], 0, 2048), R("off", oo + c // 16, oo + (c + w) // 16)),
+                   R("a2e", 512 * t + c, 512 * t + c + w) if d == 0 else ec, ALU.max)
+            if d < 4:
+                if PAR["lv"][m] > d:
+                    ts(rr, ek, 1.0 / 256, ALU.mult, 144.0 - 127.5 / 256, ALU.add)
                 else:
-                    ts(R("fl", o, o + 256), R("dd", o, o + 256), 0.0, ALU.max)
-                mm([(R("h0", 256, 384), R("fl", o + 128 * x, o + 128 * x + 128), R("idn")) for x in range(2)])
-                act(R("ob", 128 * half, 128 * half + 128), R("h0", 256, 384), ACT.Sign)
+                    act(rr, ek, ACT.Identity, bias=144.0 - 127.5 / 256, scale=1.0 / 256)
+
+        def chain(mem):
+            n, m0 = len(mem), mem[0][0]
+            o, lo, hi = 32 * m0, 512 * m0, 512 * (m0 + n)
+            b, st, w = bank(), 4 * n, 32 * n
+            mm([(R(b, 0, w), R("idn"), R("cm", 0, w))] + [(R(b, r, w, st), R("e", lo + r, hi, st), R(mat, 144, 152)) for r in range(st)], stop=False)
+            mm([(R(b, r, w, st), R("rr", lo + r, hi, st), R(mat, 152, 160)) for r in range(st)], start=False)
+            hz, rep = "hz%d%d" % (n, m0 // 2), 4 // n
+            ts(R("q4", o, o + w), R(b, 0, w), MAGIC, ALU.add, MAGIC, ALU.subtract)
+            tt(R(hz, 16 - st, 144 - st, rep), R(b, 0, w), R("q4", o, o + w), ALU.subtract)
+            mm([(R(b, 128, 128 + w), R("idn"), R("av", o, o + w))]
+               + [(R(b, 128, 128 + w), R(hz, 16 - st - st * k, 144 - st - st * k), R("idn", k, 128, rep)) for k in range(rep)])
+            act(R(b, 256, 256 + w), R(b, 128, 128 + w), ACT.Square)
+            rows = [5 * m + d + 1 for m, d in mem]
+            to_offsets(R(b, 256, 256 + w), R("ct", 32 * rows[0], 32 * rows[-1] + 32, rows[1] - rows[0]), o)
+            for m, d in mem:
+                if d == 3:
+                    rr = R("rr", 512 * m, 512 * m + 512)
+                    if PAR["rv"][m]:
+                        ts(rr, rr, -144.0, ALU.add, 0.0, ALU.max)
+                    else:
+                        act(rr, rr, ACT.Relu, bias=-144.0)
+
+        def verdict(m, s, ns):
+            k = nblk[0] % NROT; nblk[0] += 1
+            w, at = 512 // ns, done_order.index(m)
+            pb = R(bank(), 0, w)
+            mk = [R("mk", 1536 * k + 512 * x, 1536 * k + 512 * x + w) for x in range(3)]
+            dec = [(pb, R("idn"), R("e", 512 * m + s, 512 * m + 512, ns)), (pb, R("nk"), R("rr", 512 * m + s, 512 * m + 512, ns))]
+            if PAR["clamp"][at]:
+                lanes = [R("ll", 512 * x + s, 512 * x + 512, ns) for x in range(3)]
+                y = R("yv", 512 * k, 512 * k + w)
+                mm([(pb, R("idn"), R("of", s, 512, ns))] + dec[::-1])
+                if PAR["ev"][at]:
+                    cp_(y, pb)
+                else:
+                    act(y, pb, ACT.Identity)
+                for x, (a, z) in enumerate(((256.0, 768.0), (0.0, 512.0), (256.0, 512.0))):
+                    ts(mk[x], y, a, ALU.max, z, ALU.min)
+            else:
+                lanes = [R(bgin, s, 512, ns), R(ain, s, 512, ns), R(bgin, 512 + s, 1024, ns)]
+                mm(dec[::-1])
+                for x, z in enumerate((R("zb", s, 512, ns), R("zaj", 512 * t + s, 512 * t + 512, ns), R("zab", s, 512, ns))):
+                    tt(mk[x], pb, z, ALU.mult)
+            ao = 1536 * k
+            nl = PAR["la"][at] if PAR["clamp"][at] and ns == 1 else 0
+            if nl:
+                dadd("la%d%d" % (t, at), R("mk", ao, ao + 512 * nl), R("ll", 0, 512 * nl))
+            for x in range(2, -1, -1):
+                ub = R(bank(), 0, w)
+                mm([(ub, qq, lanes[x])] * (x >= nl) + [(ub, qq, mk[x])])
+                if x < 2 and PAR["df"][at]:
+                    act(ub, ub, ACT.Abs, bias=aim)
+                    tt(R("ab", ao + 512 * x, ao + 512 * x + w), R("ab", ao + 1024, ao + 1024 + w), ub, ALU.subtract)
+                else:
+                    act(R("ab", ao + 512 * x, ao + 512 * x + w), ub, ACT.Abs, bias=aim)
+            if s == 0:
+                dd[m] = bank()
+            for b in range(4 // ns):
+                ab = [R("ab", ao + 512 * x + b, ao + 512 * x + w, 4 // ns) for x in range(3)]
+                if PAR["df"][at]:
+                    for x in range(2):
+                        mm([(R(dd[m], 32 - 32 * x + s + ns * b, 64 - 32 * x, 4), ab[x], R("sm", 8 - 8 * x, 16 - 8 * x))])
+                else:
+                    mm([(R(dd[m], s + ns * b, 64, 4), ab[x], R("sm", 32 - 16 * x, 48 - 16 * x)) for x in range(3)])
+            if s == ns - 1:
+                fa, wb = R("fa", 32 * m, 32 * m + 32), "wb%d" % (nd[0] % NHZ)
+                if PAR["fv"]:
+                    ts(fa, R(dd[m], 32, 64), 0.0, ALU.is_gt, 4.0e6, ALU.mult)
+                else:
+                    act(fa, R(dd[m], 32, 64), ACT.Relu, scale=4.0e6)
+                tt(R(wb, 12, 140, 4), R(dd[m], 0, 32), fa, ALU.is_lt)
+                if nd[0] == 7:
+                    mm([(R(cb, 32 * x, 32 * x + 32), R("idn"), R("lsin%d" % t, 0, 32)) for x in range(2)], start=False, stop=False)
+                mm([(R(cb, 0, 64), R("idn"), R("cm", 64, 128))] * (nd[0] == 0)
+                   + [(R(cb, 0, 64), R(wb, 12 - 4 * r, 140 - 4 * r), R("pick", 64 * r, 64 * r + 64)) for r in range(4)],
+                   start=nd[0] == 0, stop=nd[0] == 7)
+                nd[0] += 1
 
         for d in range(1, 4):
-            ev.append((d - 1.01, lambda d=d: tables(d)))
+            ev.append((-9 + d, d + PAR["tb"], lambda d=d: tables(d)))
         if t == 1:
-            ev.append((0.5, lambda: (tables(4), store("Y", "y0", R("raw", 0, 512)))))
+            ev.append((-5, PAR["pa"] - 0.1, lambda: tables(4)))
         if t == 0:
-            ev.append((PAR["pro"], lambda: prologue(1)))
-            ev.append((PAR["f1"], lambda: first_lanes(1, "h1")))
-        ev.append((PAR["pa"], partners))
-        ev.append((PAR["ma"], masks))
-        for c in range(len(sz)):
+            ev.append((29, PAR["ah"], ahead))
+            ev.append((30, PAR["pro"], lambda: prologue(1)))
+            ev.append((-4, PAR["f0"], lambda: first_lanes(0)))
+            ev.append((31, PAR["f1"], lambda: first_lanes(1)))
+        ev.append((-3, PAR["pa"], partners))
+        ev.append((-2, PAR["ma"], masks))
+        for p, mem in wv:
+            ev.append((p + 0.001, p + PAR["ch"], lambda mem=mem: chain(mem)))
+        for m in range(8):
             for d in range(5):
-                ev.append((d + PAR["sig"][c], lambda c=c, d=d: step(c, d)))
-            for mb in range(sz[c]):
-                ns = PAR["ns"][m0[c] + mb]
-                for s in range(ns):
-                    ev.append((PAR["vo"] + PAR["sig"][c] + PAR["vd"] * (mb + s / ns), lambda c=c, mb=mb, s=s, ns=ns: verdict(c, mb, s, ns)))
+                ev.append((pos[m] + d, pos[m] * (PAR["s0"] if d == 0 else 1) + d, lambda m=m, d=d: step(m, d)))
+            ns = PAR["ns"][done_order.index(m)]
+            for s in range(ns):
+                ev.append((pos[m] + 4.002, pos[m] + 4 + PAR["vo"] + 0.01 * s, lambda m=m, s=s, ns=ns: verdict(m, s, ns)))
         ev.sort(key=lambda x: x[0])
-        for v, f in ev:
+        for _, v, f in ev:
             pr[0] = P0 + v
             f()
         pr[0] = P0 + 20
-        for k in range(2):
-            mm([(R("h1", 32 * k, 32 * k + 32), R("fp", 12 - 4 * r, 140 - 4 * r), R("ob", 128 * x + r, 128 * x + 128, 4)) for x in range(2) for r in range(4)])
-        act(R("cnt%d" % t), R("h1", 0, 64), ACT.Identity)
-        send("cnt%d" % t, R("cnt%d" % t), R("cntin%d" % t), -1 - t)
+        tt(R("zz", 0, 64), R(cb, 0, 64), R("base"), ALU.min)
+        tt(R("zz", 64, 128), R("zz", 0, 64), R("lsin%d" % t, 32, 96), ALU.max)
+        cp_(R("uo%d" % t), R("zz", 64, 128))
+    send("uo", R("uo1"), R("uoin"), 1)
     pr[0] = 140
-    tt(R("ac"), R("cntin1"), R("thr", 64, 128), ALU.is_lt)
-    tt(R("ad"), R("ac"), R("dif", 64, 128), ALU.mult)
-    tt(R("ae"), R("ad"), R("base"), ALU.add)
-    cp_(R("uoff"), R("ae"))
-    cp_(IND(R("raw", 1024, 2560), R("uoff", 0, 32)), R("donin1"))
-    act(R("ya"), IND(R("bg1", 512, 1536), R("uoff", 32, 64)), ACT.Copy)
+    cp_(IND(R("back", 1024, 2560), R("uoin", 0, 32)), R("donin"))
+    act(R("ya"), IND(R("w1"), R("uoin", 32, 64)), ACT.Copy)
     store("S", "y1", R("ya"), 512)
-    store("Y", "y2", R("raw", 1024, 1536))
-    store("S", "y3", R("raw", 1536, 2048))
+    store("Y", "y2", R("back", 1024, 1536))
+    store("S", "y3", R("back", 1536, 2048))
     return ops
 
 
-def schedule(ops):
-    hist = {}
+def depend(ops):
+    hist, lease = {}, {}
     for i, o in enumerate(ops):
-        if "deps" in o:
-            break
-        deps = {}
-        hard = set()
+        deps, hard = {}, set()
         acc = [(a, False) for a in o["rd"]] + [(a, True) for a in o["wr"]]
         for a, w in acc:
-            bank = a[0] in BANKS
             for j, lo, hi, wj in hist.get(a[0], []):
                 if j == i:
                     continue
-                if bank:
-                    deps[j] = deps.get(j, False) or (wj and not w)
-                elif lo < a[2] and a[1] < hi and (w or wj):
-                    deps[j] = deps.get(j, False) or (wj and not w)
+                meet = lo < a[2] and a[1] < hi and (w or wj)
+                if leased(a[0]):
+                    if meet or ops[j]["eng"] != o["eng"] or j == lease[a[0]][0]:
+                        deps[j] = deps.get(j, False) or (wj and not w)
+                        if meet and o["eng"] != "P":
+                            hard.add(j)
+                elif meet:
+                    deps[j] = deps.get(j, False) or wj
                     hard.add(j)
+        for j in range(i if "after" in o else 0):
+            if ops[j]["name"] in o["after"]:
+                deps[j] = False
         o["hard"] = hard
+        o["takes"] = None
+        o["banks"] = set(a[0] for a, w in acc if leased(a[0]))
+        for k in o["banks"]:
+            if k not in lease:
+                o["takes"] = k
+            lease.setdefault(k, []).append(i)
         for a, w in acc:
             h = hist.setdefault(a[0], [])
-            if a[0] in BANKS:
-                if h and h[-1][0] != i and ops[h[-1][0]]["eng"] != o["eng"]:
-                    del h[:]
-            elif w and a[3] == 1:
+            if w and a[3] == 1 and not leased(a[0]):
                 h[:] = [x for x in h if not (a[1] <= x[1] and x[2] <= a[2])]
             h.append((i, a[1], a[2], w))
         o["deps"] = deps
+    return lease
+
+
+def schedule(ops, shift=None):
+    if "lease" not in ops[0]:
+        ops[0]["lease"] = depend(ops)
+        for o in ops:
+            o["base"] = (o["deps"], o["hard"])
+    lease = ops[0]["lease"]
+    for o in ops:
+        o["deps"], o["hard"] = dict(o["base"][0]), set(o["base"][1])
+    LAT = COST["lat"]
     n = len(ops)
     users = [[] for _ in range(n)]
     left = [len(o["deps"]) for o in ops]
@@ -511,7 +644,7 @@ def schedule(ops):
     below = [0.0] * n
     for i in range(n - 1, -1, -1):
         below[i] = ops[i]["cost"] + ops[i]["lat"] + LAT + max([below[u] for u in users[i]] + [0.0])
-    key = [ops[i]["prio"] * PAR["w"] - below[i] + 500.0 * NUDGE.get(i, 0) for i in range(n)]
+    key = [ops[i]["prio"] * PAR["w"] - PAR["cp"] * below[i] + (shift[i] if shift else 0.0) for i in range(n)]
     ready = {e: [] for e in "VSPGY"}
     rt = [0.0] * n
     for i in range(n):
@@ -519,32 +652,156 @@ def schedule(ops):
             ready[ops[i]["eng"]].append(i)
     free = {e: 0.0 for e in "VSPGY"}
     order = {e: [] for e in "VSPGY"}
-    end = 0.0
+    idle = [(0.0, b, None) for b in BANKS]
+    todo = {k: len(v) for k, v in lease.items()}
+    until = {k: 0.0 for k in lease}
+    end, link = 0.0, [0.0, 0.0]
     for _ in range(n):
         best = None
         for e in "VSPGY":
-            if not ready[e]:
+            can = [(max(rt[i], idle[0][0]) if ops[i]["takes"] else rt[i], i) for i in ready[e] if idle or not ops[i]["takes"]]
+            if not can:
                 continue
-            t0 = max(free[e], min(rt[i] for i in ready[e]))
-            i = min((i for i in ready[e] if rt[i] <= t0 + PAR["look"]), key=lambda i: (key[i], i))
-            t0 = max(t0, rt[i])
+            t0 = max(free[e], min(can)[0])
+            r, i = min((c for c in can if c[0] <= t0 + PAR["look"]), key=lambda c: (key[c[1]], c[1]))
+            t0 = max(t0, r)
             if best is None or t0 < best[0]:
                 best = (t0, e, i)
         t0, e, i = best
         ready[e].remove(i)
         order[e].append(i)
         o = ops[i]
+        if o["takes"]:
+            _, b, before = idle.pop(0)
+            MAP[o["takes"]] = b
+            for j in lease.get(before, []):
+                o["deps"].setdefault(j, False)
+                if e != "P":
+                    o["hard"].add(j)
         o["t0"] = t0
         free[e] = t0 + o["cost"]
         done = free[e] + o["lat"]
+        if o["kind"] == "send":
+            done = landed(o, link, free[e])
         end = max(end, done)
+        for k in o["banks"]:
+            todo[k] -= 1
+            until[k] = max(until[k], done + LAT)
+            if todo[k] == 0:
+                idle.append((until[k], MAP[k], k))
+                idle.sort()
         for u in users[i]:
-            same = ops[u]["eng"] == e and o["kind"] == "c" and i not in ops[u]["hard"]
-            rt[u] = max(rt[u], free[e] if same else done + LAT)
+            same = ops[u]["eng"] == e and o["kind"] == "c"
+            rt[u] = max(rt[u], done + (LAT if not same else COST["own"] if i in ops[u]["hard"] else 0.0))
             left[u] -= 1
             if left[u] == 0:
                 ready[ops[u]["eng"]].append(u)
+    key = [o["t0"] for o in ops]
+    best = None
+    for _ in range(PASSES):
+        order, end = forward(ops, users, key)
+        if best is None or end < best[0]:
+            best = (end, key)
+        key = backward(ops)
+    return forward(ops, users, best[1])
+
+
+def slot(S, E, t, c):
+    lo, hi = 0, len(E)
+    while lo < hi:
+        if E[(lo + hi) // 2] <= t:
+            lo = (lo + hi) // 2 + 1
+        else:
+            hi = (lo + hi) // 2
+    while lo < len(S) and S[lo] < t + c:
+        t = max(t, E[lo])
+        lo += 1
+    S.insert(lo, t)
+    E.insert(lo, t + c)
+    return lo, t
+
+
+def landed(o, link, t):
+    k = int(o["name"] in RELAYED)
+    link[k] = max(link[k], t + 5000 * k) + o["lat"] - 1800
+    return link[k] + 1800 + (0 if o["name"] in ("a0", "uo") else 4000)
+
+
+def wake(p, o, hard):
+    return COST["lat"] if p["eng"] != o["eng"] or p["kind"] != "c" else COST["own"] if hard else 0.0
+
+
+def forward(ops, users, key):
+    lease = ops[0]["lease"]
+    for o in ops:
+        o["deps"], o["hard"] = dict(o["base"][0]), set(o["base"][1])
+    left = [len(o["deps"]) for o in ops]
+    rt = [0.0] * len(ops)
+    ready = [i for i in range(len(ops)) if left[i] == 0]
+    S, E, order = [{e: [] for e in "VSPGY"} for _ in range(3)]
+    idle = [(0.0, b, None) for b in BANKS]
+    todo = {k: len(v) for k, v in lease.items()}
+    until = {k: 0.0 for k in lease}
+    end, link = 0.0, [0.0, 0.0]
+    while ready:
+        i = min((j for j in ready if idle or not ops[j]["takes"]), key=lambda j: (key[j], j))
+        ready.remove(i)
+        o = ops[i]
+        e, t = o["eng"], rt[i]
+        if o["takes"]:
+            can = [x for x in idle if x[0] <= t]
+            x = max(can) if can else min(idle)
+            idle.remove(x)
+            t = max(t, x[0])
+            MAP[o["takes"]] = x[1]
+            for j in lease.get(x[2], []):
+                o["deps"].setdefault(j, False)
+                if e != "P":
+                    o["hard"].add(j)
+        if e in "GY" and E[e]:
+            t = max(t, E[e][-1])
+        k, t = slot(S[e], E[e], t, o["cost"])
+        order[e].insert(k, i)
+        o["t0"] = t
+        done = t + o["cost"] + o["lat"]
+        if o["kind"] == "send":
+            done = landed(o, link, t + o["cost"])
+        o["done"] = done
+        end = max(end, done)
+        for b in o["banks"]:
+            todo[b] -= 1
+            until[b] = max(until[b], done + COST["lat"])
+            if todo[b] == 0:
+                idle.append((until[b], MAP[b], b))
+        for u in users[i]:
+            rt[u] = max(rt[u], done + wake(o, ops[u], i in ops[u]["hard"]))
+            left[u] -= 1
+            if left[u] == 0:
+                ready.append(u)
     return order, end
+
+
+def backward(ops):
+    left = [0] * len(ops)
+    for o in ops:
+        for j in o["deps"]:
+            left[j] += 1
+    rt = [0.0] * len(ops)
+    key = [0.0] * len(ops)
+    ready = [i for i in range(len(ops)) if left[i] == 0]
+    S, E = [{e: [] for e in "VSPGY"} for _ in range(2)]
+    while ready:
+        i = min(ready, key=lambda j: (-ops[j]["done"], j))
+        ready.remove(i)
+        o = ops[i]
+        t = slot(S[o["eng"]], E[o["eng"]], rt[i] + o["done"] - o["t0"] - o["cost"], o["cost"])[1] + o["cost"]
+        key[i] = -t - (PAR["early"] if o["eng"] in "GY" else 0.0)
+        for j in o["deps"]:
+            rt[j] = max(rt[j], t + wake(ops[j], o, j in o["hard"]))
+            left[j] -= 1
+            if left[j] == 0:
+                ready.append(j)
+    return key
 
 
 PLAN = {}
@@ -552,14 +809,34 @@ PLAN = {}
 
 def rank_program(g, core, T, topo):
     rank = T.rank_of(core)
-    if rank is None:
+    cores = T.cores
+    n = len(cores)
+    helper = [[c for c in topo.cores_of(x) if topo.die(c) != topo.die(x)][0] for x in cores]
+    if rank is None and core not in helper:
         return
     if not PLAN:
         PLAN["ops"] = build()
         PLAN["order"], PLAN["end"] = schedule(PLAN["ops"])
     ops, order = PLAN["ops"], PLAN["order"]
-    cores = T.cores
-    n = len(cores)
+
+    def inner(r, hop):
+        out = topo.engines(cores[r], cores[(r + hop) % n])
+        return [x for x in topo.engines(cores[r], helper[r]) if x not in out]
+
+    if rank is None:
+        r = helper.index(core)
+        for i in order["G"]:
+            o = ops[i]
+            if o["name"] in RELAYED:
+                src, dst, hop = o["fn"]
+                peer = cores[(r + hop) % n]
+                rid, pid = topo.addr(peer, core)
+                g.wait_ge(T.sem["r_" + o["name"]], len(inner(r, hop)))
+                g.remote_dma(ap(T, dst), ap(T, dst), T.sem["r_" + o["name"]], T.sem["l_" + o["name"]], pid, rid, topo.mask(core, peer))
+        for i in order["G"]:
+            if ops[i]["name"] in RELAYED:
+                g.wait_ge(T.sem["l_" + ops[i]["name"]], len(topo.engines(core, cores[(r + ops[i]["fn"][2]) % n])))
+        return
     queue = {"V": g.vector, "S": g.scalar, "P": g.tensor, "G": g, "Y": g.sync}
     count = {}
     total = {}
@@ -575,8 +852,9 @@ def rank_program(g, core, T, topo):
             total["d_" + o["name"]] = 16
         elif o["kind"] == "send":
             hop = o["fn"][2]
-            total["l_" + o["name"]] = len(topo.engines(core, cores[(rank + hop) % n]))
-            total["r_" + o["name"]] = len(topo.engines(cores[(rank - hop) % n], core))
+            relayed = o["name"] in RELAYED
+            total["l_" + o["name"]] = len(inner(rank, hop) if relayed else topo.engines(core, cores[(rank + hop) % n]))
+            total["r_" + o["name"]] = len(topo.engines((helper if relayed else cores)[(rank - hop) % n], core))
     for e in "YSPVG":
         q = queue[e]
         seen = {}
@@ -605,9 +883,11 @@ def rank_program(g, core, T, topo):
                 o["fn"](g, T).then_inc(T.sem["d_" + o["name"]], 16)
             else:
                 src, dst, hop = o["fn"]
-                peer = cores[(rank + hop) % n]
+                relayed = o["name"] in RELAYED
+                peer = helper[rank] if relayed else cores[(rank + hop) % n]
+                mask = sum(1 << x for x in inner(rank, hop)) if relayed else topo.mask(core, peer)
                 rid, pid = topo.addr(peer, core)
-                g.remote_dma(ap(T, dst), ap(T, src), T.sem["r_" + o["name"]], T.sem["l_" + o["name"]], pid, rid, topo.mask(core, peer))
+                g.remote_dma(ap(T, dst), ap(T, src), T.sem["r_" + o["name"]], T.sem["l_" + o["name"]], pid, rid, mask)
         if e == "G":
             for s, v in total.items():
                 if seen.get(s, 0) < v:

from concourse.bass import DstId, RemoteDMATransfer
from concourse.mybir import dt, AluOpType as ALU, AxisListType, ActivationFunctionType as ACT

BF, F32, F16, I32, U16 = "bfloat16", "float32", "float16", "int32", "uint16"
NROT = 4
SB = {
    "raw": (2048, BF), "t0": (2048, F32), "t1": (2048, F32), "t2": (2048, F32), "t3": (2048, F32),
    "raw2": (2048, BF), "u0": (2560, F32), "u1": (2048, F32), "u2": (2048, F32), "u3": (2048, F32), "back": (2560, BF), "w1": (1024, BF),
    "e": (4096, F16), "rr": (4096, BF), "sg": (2048, BF),
    "ain0": (512, BF), "ain1": (512, BF), "a2e": (1024, BF), "ya": (512, BF), "na": (1024, BF),
    "bg0": (1024, BF), "bg1": (1024, BF), "bgin0": (1024, BF), "bgin1": (1024, BF), "gw": (1024, F32),
    "don0": (512, F32), "don1": (512, BF), "donin": (512, BF),
    "ls0": (64, F16), "ls1": (64, F16), "lsin0": (96, F16), "lsin1": (96, F16),
    "zaj": (1024, BF), "zb": (512, BF), "zab": (512, BF), "of": (512, BF), "ll": (1536, F16),
    "yv": (512 * NROT, F16), "mk": (1536 * NROT, F16), "ab": (1536 * NROT, F32),
    "nk": (128, BF), "pk": (128, BF), "p5": (128, BF), "n7": (128, BF),
    "cw": (32, F32), "nt": (64, F32), "fa": (256, F32), "pick": (256, BF), "zz": (128, F32),
    "hwi": (1, I32), "gli": (1, I32), "mx": (16, BF), "wf0": (4, F32), "wf1": (4, F32), "wi": (2, I32),
    "one": (128, BF), "idn": (128, BF), "nid": (128, BF), "blk": (128, BF), "upp": (128, BF), "b8": (8, F32), "b8a": (8, F32),
    "mat0": (288, BF), "mat1": (288, BF), "sp": (144, BF),
    "sm": (48, F32), "cm": (128, BF), "av": (256, BF),
    "x16": (16, I32), "x15": (16, I32), "e16": (16, F32), "pc": (4, F32),
    "ct": (1280, F32),
    "ch": (512, F32), "dum": (64, F32), "du0": (64, F32), "base": (64, F32), "la0": (32, F32),
    "q4": (384, F32), "ss": (384, F32), "sq": (64, F32), "sh": (32, F16), "ni": (576, I32), "hi": (576, I32), "off": (576, U16),
    "boff": (64, U16), "boin": (32, U16), "soff": (64, U16), "uo0": (64, U16), "uo1": (64, U16), "uoin": (64, U16),
    "bv": (64, F16), "bm": (1024, F16), "eq": (1536, BF), "sf": (64, F32), "nd": (64, F32), "pi": (64, I32), "pj": (64, I32),
    "tp": (64, F32), "ff": (32, F32), "ft0": (1056, F32), "ft1": (1056, F32), "fg": (512, BF),
}
ROWS = {"ct": 32}
NHZ = 4
for _k in range(NHZ):
    for _n in (2, 4) if _k % 2 == 0 else (2,):
        SB["hz%d%d" % (_n, _k)] = (144, F16)
        ROWS["hz%d%d" % (_n, _k)] = 4 * _n
    SB["wb%d" % _k] = (144, BF)
    ROWS["wb%d" % _k] = 4
BANKS = ["pb%d" % _k for _k in range(8)]
SCRATCH = {k: ("sbuf", [128, v[0] // ROWS[k], ROWS[k]] if k in ROWS else [128, v[0]], v[1]) for k, v in SB.items()}
for _b in BANKS:
    SCRATCH[_b] = ("psum", [128, 512], F32)
DMAS = ["la0", "la1", "lb", "lhw", "lgl", "lmx", "y0", "y1", "y2", "y3", "lw", "t010", "t020", "t030"] + ["t1%d%d" % (_d, _k) for _d in (1, 2, 3) for _k in range(3)] + ["la%d%d" % (_t, _k) for _t in range(2) for _k in range(8)]
RELAYED = ["tab2", "tab3", "tab0", "back1"]
SENDS = ["a0", "a1", "mat", "wf", "tab0", "tab1", "tab2", "tab3", "bo", "ls0", "ls1", "bg0", "bg1", "ab1", "back0", "back1", "don", "uo"]
SEMAPHORES = ["eV", "eS", "eP", "eG"] + ["d_" + k for k in DMAS] + ["r_" + k for k in SENDS] + ["l_" + k for k in SENDS]

PAR = {'trains': [[0, 1], [2, 3], [4, 5], [6, 7]], 'lag': [0, 0, 0, 0, 0, 0, 0, 0], 'sig': [-0.44, 1.86, 3.48, 3.09], 'look': 102.67, 'w': 1510.93, 'cp': 0.83, 'ns': [1, 1, 1, 1, 1, 1, 1, 2], 'clamp': [1, 1, 0, 0, 0, 0, 0, 0], 'rv': [0, 0, 0, 0, 0, 0, 0, 1], 'ev': [0, 0, 0, 0, 0, 0, 0, 0], 'lv': [0, 0, 0, 0, 0, 0, 0, 0], 'zv': 0, 's0': 0.41, 'ch': -0.83, 'vo': -1.14, 'pa': -4.01, 'ma': 4.7, 'f0': 5.83, 'pro': 12.04, 'f1': 9.17, 'own': -5.1, 'tb': 0.79, 'snd': -4.98, 'ah': -2.34, 'fv': 1, 'abv': 1, 'dt': [0, 0, 1, 0, 1, 1], 'la': [0, 0, 0, 0, 0, 0, 0, 0], 'df': [0, 0, 0, 0, 0, 1, 1, 1], 'early': 0.0, 'av': [1, 1], 'fs': [1, 1], 'hs': [0, 0, 0, 0, 0]}
MAGIC = float(3 * 2 ** 34)
COST = {"cv": 0.83, "cp": 0.42, "ga": 1.35, "sc": 3.8, "lat": 220.0, "own": 200.0, "mm": 0.0, "bw": 45.0, "add": 120.0, "xS": 1.0, "fS": 0.0, "xV": 1.0, "fV": 0.0}
PASSES = 4
MAP = {}


def R(name, lo=0, hi=None, st=1):
    return (name, lo, SB[name][0] if hi is None and name in SB else (512 if hi is None else hi), st)


def IND(win, off):
    return ("ind", win, off)


def n_of(a):
    if a[0] == "ind":
        return 16 * n_of(a[2])
    if a[0] in ROWS:
        w = ROWS[a[0]]
        return w * len(range(a[1] // w, a[2] // w, a[3]))
    return (a[2] - a[1] + a[3] - 1) // a[3]


def two(a):
    return a[0] in SB and SB[a[0]][1] in (BF, F16, U16)


def leased(name):
    return name[0] == "~"


def ap(T, a):
    if not isinstance(a, tuple):
        return a
    if a[0] == "ind":
        return ap(T, a[1]).indirect(ap(T, a[2]))
    if a[0] in ROWS:
        w = ROWS[a[0]]
        return T[a[0]][:, a[1] // w:a[2] // w:a[3], :]
    name = MAP.get(a[0], a[0])
    if a[3] == 1:
        return T[name][:, a[1]:a[2]]
    return T[name][:, a[1]:a[2]:a[3]]


def parts(a):
    if not isinstance(a, tuple):
        return []
    if a[0] == "ind":
        return [a[1], a[2]]
    return [a]


def waves():
    out = []
    for k, tr in enumerate(PAR["trains"]):
        for w in range(20):
            now = [(m, w - PAR["lag"][m]) for m in tr if 0 <= w - PAR["lag"][m] < 4]
            while now:
                n = 4 if len(now) == 4 else 2 if len(now) > 1 and now[1][0] == now[0][0] + 1 else 1
                out.append((w + PAR["sig"][k], now[:n]))
                now = now[n:]
    return out


def build():
    ops = []
    pr = [0.0]
    nb = [0]
    CV, CP, GA, SC = COST["cv"], COST["cp"], COST["ga"], COST["sc"]

    def bank():
        nb[0] += 1
        return "~%d" % nb[0]

    def add(eng, fn, rd, wr, cost, kind="c", name=None, lat=0.0):
        r2 = [x for a in rd for x in parts(a)]
        w2 = []
        for a in wr:
            if a[0] == "ind":
                w2.append(a[1]); r2.append(a[2])
            else:
                w2.append(a)
        if kind == "c" and eng in "SV":
            cost = cost * COST["x" + eng] + COST["f" + eng]
        ops.append({"eng": eng, "fn": fn, "rd": r2, "wr": w2, "cost": cost, "kind": kind, "name": name, "prio": pr[0], "lat": lat})

    def vcost(out, ins, base):
        n = n_of(out)
        if out[0] == "ind":
            return 50 + CV * SC * n
        if ins[0][0] == "ind":
            return 50 + CV * GA * n
        return CV * max(64, base * n)

    def cp_(out, a):
        add("V", lambda g, T: g.vector.tensor_copy(ap(T, out), ap(T, a)), [a], [out],
            vcost(out, [a], 0.5 if a[0] != "ind" and out[0] != "ind" and two(a) and two(out) else 1))

    def ts(out, a, s1, op0, s2=None, op1=None):
        def fn(g, T):
            if op1 is None:
                return g.vector.tensor_scalar(ap(T, out), ap(T, a), ap(T, s1), None, op0)
            return g.vector.tensor_scalar(ap(T, out), ap(T, a), ap(T, s1), ap(T, s2), op0, op1)
        add("V", fn, [a, s1, s2], [out], vcost(out, [a], 0.5 if two(a) and two(out) else 1))

    def tt(out, a, b, op):
        add("V", lambda g, T: g.vector.tensor_tensor(ap(T, out), ap(T, a), ap(T, b), op), [a, b], [out],
            vcost(out, [a], 1 if leased(a[0]) or leased(b[0]) else 2))

    def ms(out, c):
        add("V", lambda g, T: g.vector.memset(ap(T, out), c), [], [out], CV * max(64, n_of(out) * (0.5 if two(out) else 1)))

    def act(out, a, f, bias=0.0, scale=1.0):
        add("S", lambda g, T: g.scalar.activation(ap(T, out), ap(T, a), f, bias=ap(T, bias), scale=ap(T, scale)), [a, bias, scale], [out],
            (65 + CV * GA * n_of(out)) if a[0] == "ind" else CV * max(64, n_of(out)))

    def mm(lst, start=True, stop=True):
        def fn(g, T):
            ins = None
            for i, (o, l, r) in enumerate(lst):
                ins = g.tensor.matmul(ap(T, o), ap(T, l), ap(T, r), start and i == 0, stop and i == len(lst) - 1)
            return ins
        c = sum(max(min(64, n_of(l)), n_of(r)) * (4 if SB[l[0]][1] == F32 else 1) for o, l, r in lst)
        add("P", fn, [x for o, l, r in lst for x in (l, r)], [o for o, l, r in lst], CP * c + COST["mm"] * len(lst))

    def iota(out, pat, base, cm=0):
        if SB[out[0]][1] == I32:
            add("G", lambda g, T: g.iota(ap(T, out), pat, base, cm), [], [out], 130 + 2 * CV * n_of(out))
        else:
            add("G", lambda g, T: g.iota(ap(T, out), pat, base, cm, allow_small_or_imprecise_dtypes=True), [], [out], 130 + 2 * CV * n_of(out))

    def sel(out, a, pat, op, base, cm):
        add("G", lambda g, T: g.affine_select(ap(T, out), ap(T, a), pat, op, 0.0, base, cm), [a], [out], 170 + 2 * CV * n_of(out))

    def load(eng, name, out, src):
        def fn(g, T):
            q = g.sync if eng == "Y" else g.scalar
            return q.dma_start(ap(T, out), src(T))
        add(eng, fn, [], [out], 100, "dma", name, 1800 + n_of(out) * 1.0)

    def store(eng, name, a, at=None):
        at = a[1] if at is None else at

        def fn(g, T):
            q = g.sync if eng == "Y" else g.scalar
            return q.dma_start(T.y[:, at:at + n_of(a)], ap(T, a))
        add(eng, fn, [a], [], 100, "dma", name, 1800 + n_of(a) * 1.0)

    def send(name, src, dst, hop):
        add("G", (src, dst, hop), [src], [dst], 800, "send", name, 1800 + n_of(src) * (2 if two(src) else 4) * 128 / COST["bw"])

    def dadd(name, out, a):
        add("G", lambda g, T: g.dma_start(ap(T, out), ap(T, a), accum_op=ALU.add), [a, out], [out], 1000, "dma", name,
            2200 + n_of(a) * (2 if two(a) else 4) * 128 / COST["add"])

    def empty(out, a):
        if PAR["zv"]:
            ts(out, a, 0.0, ALU.is_equal)
        else:
            act(out, a, ACT.Relu, bias=1.0, scale=-1.0)

    pr[0] = -10
    load("Y", "la0", R("raw", 0, 512), lambda T: T.ent[:, 0:512])
    load("S", "lb", R("raw", 1024, 2048), lambda T: T.ent[:, 1024:2048])
    load("Y", "lhw", R("hwi"), lambda T: T.hw[:])
    load("Y", "la1", R("raw", 512, 1024), lambda T: T.ent[:, 512:1024])
    load("S", "lmx", R("mx"), lambda T: T.mix[:])
    load("Y", "lgl", R("gli"), lambda T: T.goal[:])
    send("a0", R("raw", 0, 512), R("ain0"), 1)
    pr[0] = -9
    ms(R("one"), 1.0)
    iota(R("x16"), [[-1, 16]], 16, 1)
    sel(R("b8a"), R("one", 0, 8), [[-16, 8]], ALU.is_ge, 0, 1)
    sel(R("b8"), R("b8a"), [[16, 8]], ALU.is_ge, 15, -1)
    sel(R("idn"), R("one"), [[-1, 128]], ALU.is_equal, 0, 1)
    ms(R("mat0", 0, 144), 0.0)
    ms(R("sp"), 0.0)
    ms(R("wf0"), 0.0)
    ms(R("cm", 0, 64), -2048.0)
    ms(R("cm", 64, 128), 4096.0)
    ts(R("x15"), R("x16"), 15, ALU.bitwise_and)
    ts(R("e16"), R("x15"), 0.0, ALU.is_equal)
    cp_(R("pc", 0, 1), R("x15", 0, 1))
    ts(R("nid"), R("idn"), -1.0, ALU.mult)
    cp_(R("wf0", 0, 1), R("hwi"))
    ts(R("wi", 0, 1), R("hwi"), 15, ALU.bitwise_and)
    cp_(R("wf0", 1, 2), R("wi", 0, 1))
    ts(R("mat0", 15, 143, 16), R("b8"), R("wf0", 0, 1), ALU.mult)
    ts(R("mat0", 144, 152), R("b8"), R("wf0", 0, 1), ALU.mult)
    ts(R("mat0", 152, 160), R("b8"), R("wf0", 1, 2), ALU.mult, -256.0, ALU.mult)
    for m in range(8):
        ms(R("ct", 160 * m, 160 * m + 32), -256.0 * (2 * m + 1) ** 2)
    for d in range(1, 5):
        act(R("ct", 32 * d, 1280, 5), R("ct", 0, 1280, 5), ACT.Identity, bias=32.0 * 811 * d)
    iota(R("av"), [[32, 8], [0, 32]], 2064)
    sel(R("upp"), R("one"), [[-16, 8], [0, 16]], ALU.is_ge, 0, 1)
    sel(R("blk"), R("upp"), [[16, 8], [0, 16]], ALU.is_ge, 15, -1)
    pr[0] = -8
    for k in (0, 2, 3, 1):
        lo, b = 512 * k, bank()
        ts(R("sg", lo, lo + 512), R("raw", lo, lo + 512), 0.0, ALU.is_gt, 2048.0, ALU.mult)
        mm([(R(b), R("idn"), R("raw", lo, lo + 512)), (R(b), R("idn"), R("sg", lo, lo + 512))])
        act(R("t0", lo, lo + 512), R(b), ACT.Identity, bias=-1024.0)
    pr[0] = -7
    for name in sorted(set("hz%d%d" % (len(w[1]), w[1][0][0] // 2) for w in waves() if len(w[1]) < 4)) + ["wb%d" % k for k in range(NHZ)]:
        ts(R(name), R("mat0", 0, 144), 0.0, ALU.mult)
    sel(R("upp"), R("blk"), [[1, 128]], ALU.is_gt, 0, -1)
    iota(R("du0"), [[0, 32], [16, 2]], 1025)
    iota(R("la0"), [[16, 32]], 0)
    iota(R("ch"), [[1, 16], [0, 32]], 20)
    iota(R("ft0"), [[0, 1056]], 0)

    pr[0] = -6
    b = bank()
    mm([(R(b, 0, 64), R("idn"), R("cm", 0, 64))] + [(R(b, 0, 64), R("mat0", 15 - r, 143 - r), R("raw", r, 1024, 16)) for r in range(16)])
    ts(R("q4", 256, 320), R(b, 0, 64), MAGIC, ALU.add, MAGIC, ALU.subtract)
    tt(R("ss", 256, 320), R(b, 0, 64), R("q4", 256, 320), ALU.subtract)
    act(R("sq"), R("ss", 256, 320), ACT.Square, bias=2048.0 + 592)
    ts(R("ni", 256, 320), R("sq"), -592.0 * 592, ALU.add)
    ts(R("hi", 256, 320), R("ni", 256, 320), 5, ALU.arith_shift_right, 1023, ALU.bitwise_and)
    cp_(R("boff"), R("hi", 256, 320))
    ts(R("bv"), R("hi", 256, 320), 1.0, ALU.add)
    pr[0] = PAR["own"]
    for r in range(16):
        ts(R("bm", 64 * r, 64 * r + 64), R("bv"), R("e16", r, r + 1), ALU.mult)
    for k in range(2):
        b = bank()
        mm([(R(b), R("upp"), R("bm", 512 * k, 512 * k + 512))] + [(R(b, 64 * r, 64 * r + 64), R("nid"), R("bv")) for r in range(8)])
        ts(R("eq", 512 * k, 512 * k + 512), R(b), 0.0, ALU.is_equal, 2048.0, ALU.mult)
    b = bank()
    mm([(R(b), R("blk"), R("bm", 0, 1024, 2))] + [(R(b, 32 * r, 32 * r + 32), R("nid"), R("bv", 1, 64, 2)) for r in range(16)])
    ts(R("eq", 1024, 1536), R(b), 0.0, ALU.is_equal, 2048.0, ALU.mult)
    b = bank()
    mm([(R(b, 0, 64), R("idn"), R("bv"))] + [(R(b, 0, 64), R("idn"), R("eq", 64 * r, 64 * r + 64)) for r in range(16)]
       + [(R(b, 1, 64, 2), R("idn"), R("eq", 1024 + 32 * r, 1056 + 32 * r)) for r in range(16)])
    ts(R("dum"), R("du0"), R("pc", 0, 1), ALU.add)
    tt(R("sf"), R(b, 0, 64), R("dum"), ALU.min)
    ts(R("soff"), R("sf"), -1.0, ALU.add)
    ts(R("nd"), R("sf"), 1024.5, ALU.is_lt)
    ts(R("pi"), R("ss", 256, 320), 2048.0, ALU.add)
    ts(R("pj"), R("pi"), 1, ALU.bitwise_and)
    ts(R("tp"), R("pj"), 6.5, ALU.add, -4096.0, ALU.mult)
    tt(R("nt"), R("tp"), R("nd"), ALU.mult)
    ts(R("base", 0, 32), R("la0"), R("pc", 0, 1), ALU.add, 1024.0, ALU.add)
    ts(R("base", 32, 64), R("base", 0, 32), -512.0, ALU.add)
    for t in range(2):
        cp_(R("ls%d" % t, 32, 64), R("hi", 256 + 32 * t, 288 + 32 * t))
        ts(R("lsin%d" % t, 64, 96), R("la0"), R("pc", 0, 1), ALU.add)
    cp_(R("sp", 15, 143, 16), R("b8"))
    pr[0] = -4.0
    iota(R("ft1"), [[0, 1056]], 0)
    load("Y", "lw", R("w1", 512, 1024), lambda T: T.ent[:, 512:1024])
    for a in range(8):
        act(R("mat0", 160 + 16 * a, 176 + 16 * a), R("mx"), ACT.Identity, scale=R("b8", a, a + 1))
    for k, s in (("nk", -256.0), ("pk", 256.0), ("p5", 512.0), ("n7", -768.0)):
        ts(R(k), R("idn"), s, ALU.mult)
    ms(R("pick"), 4096.0)
    sel(R("pick"), R("pick"), [[-1, 4], [0, 2], [-4, 32]], ALU.is_equal, 0, 1)
    iota(R("cw"), [[16, 16], [0, 2]], 320)
    ts(R("wf0", 2, 3), R("gli"), -1.0, ALU.mult)
    ms(R("sm"), 0.0)
    for lo, s in ((0, -1.0), (8, 1.0), (16, 1.0), (40, -1.0)):
        ts(R("sm", lo, lo + 8), R("b8"), s, ALU.mult)
    pr[0] = PAR["snd"]
    send("a1", R("raw", 512, 1024), R("ain1"), -1)
    send("mat", R("mat0"), R("mat1"), 1)
    send("wf", R("wf0"), R("wf1"), 1)
    send("bo", R("boff", 32, 64), R("boin"), 1)
    for k, name in enumerate(["t1", "t2", "t3", "u1", "u2", "u3"]):
        pr[0] = PAR["snd"] + 2 * (k // 3)
        for lo in range(0, 2048 * PAR["dt"][k], 512):
            iota(R(name, lo, lo + 512), [[0, 512]], -256 * (k % 3 + 1))
    iota(R("u0", 2048, 2560), [[0, 512]], 0)
    iota(R("back", 2048, 2560), [[0, 512]], 0)

    def first_lanes(t):
        ft, b = "ft%d" % t, bank()
        for k in range(15, -1, -1):
            out, a = IND(R(ft), R("soff", 32 * t + 2 * k, 32 * t + 2 * k + 2)), R("ch", 32 * k, 32 * k + 32)
            if PAR["fs"][t]:
                add("S", lambda g, T, out=out, a=a: g.scalar.activation(ap(T, out), ap(T, a), ACT.Silu), [a], [out], 65 + CV * SC * 32)
            else:
                cp_(out, a)
        act(R("fg"), IND(R(ft), R("boff", 32 * t, 32 * t + 32)), ACT.Copy)
        mm([(R(b, 0, 32), R("sp", 15 - r, 143 - r), R("fg", r, 512, 16)) for r in range(16)])
        tt(R("ff"), R(b, 0, 32), R("cw"), ALU.is_equal)
        tt(R("ls%d" % t, 0, 32), R("ff"), R("nt", 32 * t, 32 * t + 32), ALU.mult)
        send("ls%d" % t, R("ls%d" % t), R("lsin%d" % t, 0, 64), 1 - 2 * t)

    def to_offsets(sq, ct, o):
        w = n_of(sq)
        tt(R("ni", o, o + w), sq, ct, ALU.add)
        ts(R("hi", o, o + w), R("ni", o, o + w), 5, ALU.arith_shift_right, 2047, ALU.bitwise_and)
        cp_(R("off", o, o + w), R("hi", o, o + w))

    def prologue(t):
        ain, o, b = "ain%d" % t, 320 * t, bank()
        mm([(R(b, 0, 32), R("idn"), R("cm", 0, 32))] + [(R(b, 0, 32), R("mat%d" % t, 15 - r, 143 - r), R(ain, r, 512, 16)) for r in range(16)])
        ts(R("q4", o, o + 32), R(b, 0, 32), MAGIC, ALU.add, MAGIC, ALU.subtract)
        ss = R("sh") if t else R("ss", o, o + 32)
        tt(ss, R(b, 0, 32), R("q4", o, o + 32), ALU.subtract)
        if PAR["av"][t]:
            ts(R("a2e", 512 * t, 512 * t + 512), R(ain), -256.0, ALU.add)
        else:
            act(R("a2e", 512 * t, 512 * t + 512), R(ain), ACT.Identity, bias=-256.0)
        for ms_ in ([[0, 1], [2, 3], [4, 5, 6, 7]] if t == 0 else [list(range(8))]):
            b = bank()
            if t:
                mm([(R(b, 256, 512), R("idn"), R("av"))] + [(R(b, 256 + 32 * m, 288 + 32 * m), R("idn"), ss) for m in ms_])
                act(R(b, 0, 256), R(b, 256, 512), ACT.Square)
            for k, m in enumerate(ms_ * (1 - t)):
                act(R(b, 32 * k, 32 * k + 32), ss, ACT.Square, bias=2064.0 + 32 * m)
            to_offsets(R(b, 0, 32 * len(ms_)), R("ct", 160 * ms_[0], 160 * ms_[-1] + 32, 5), o + 32 * ms_[0])
        empty(R("zaj", 512 * t, 512 * t + 512), R(ain))

    wv = waves()
    pos = {}
    for k, tr in enumerate(PAR["trains"]):
        for m in tr:
            pos[m] = PAR["lag"][m] + PAR["sig"][k]
    done_order = sorted(range(8), key=lambda m: (pos[m], m))
    nblk = [0]
    nhz = [0]
    for t in range(2):
        P0 = 100.0 * t
        ain, bg, bgin = "ain%d" % t, "bg%d" % t, "bgin%d" % t
        zaj = R("zaj", 512 * t, 512 * t + 512)
        bo = R("boin") if t else R("boff", 0, 32)
        tabs = [["t0", "t1", "t2", "t3", "raw"], ["u0", "u1", "u2", "u3", "raw2"]]
        mat, qq, aim = "mat%d" % t, R("mat%d" % t, 160, 288), R("wf%d" % t, 2, 3)
        if t == 0:
            pr[0] = -8.5
            prologue(0)
        else:
            pr[0] = 40
            cp_(IND(R("u0", 1024, 2560), R("uo0", 0, 32)), R("don0"))
            act(R("u0", 0, 512), IND(R("gw"), R("uo0", 32, 64)), ACT.Copy)
        spans = [(0, 1024), (1024, 2048)] if t == 0 else [(0, 512), (1024, 1536), (1536, 2048)]
        ev = []
        cb = bank()
        dd = {}
        nd = [0]

        def tables(d, t=t, spans=spans):
            if d < 4 and PAR["dt"][3 * t + d - 1]:
                for lo, hi in [(0, 2048)] if t == 0 else spans if len(spans) == 1 else [(0, 512), (1024, 2048)]:
                    dadd("t%d%d%d" % (t, d, lo // 512), R(tabs[t][d], lo, hi), R(tabs[t][0], lo, hi))
                return
            for lo, hi in spans:
                if d < 4:
                    act(R(tabs[t][d], lo, hi), R(tabs[t][0], lo, hi), ACT.Identity, bias=-256.0 * d)
                else:
                    act(R(tabs[t][4], lo, hi), R(tabs[t][0], lo, hi), ACT.Relu, bias=-1024.0)

        def ahead():
            for d in range(1, 5):
                tables(d, 1, [(512, 1024)])
            b = bank()
            ts(R("ya"), R(bgin, 512, 1024), 0.0, ALU.is_gt, 2048.0, ALU.mult)
            mm([(R(b), R("idn"), R(bgin, 512, 1024)), (R(b), R("idn"), R("ya"))])
            act(R("gw", 0, 512), R(b), ACT.Identity, bias=-1024.0)

        def partners():
            A, at = (R("raw2", 512, 1024), bg) if t else (R(ain), bgin)
            act(R(bg, 0, 512), IND(R(tabs[t][4], 1024, 2048), bo), ACT.Copy)
            if t == 0:
                send(bg, R(bg, 0, 512), R(bgin, 0, 512), 1)
            b, na = bank(), R("na", 512 * t, 512 * t + 512)
            if PAR["abv"]:
                ts(na, A, 0.0, ALU.is_gt, -256.0, ALU.mult)
                mm([(R(b), R("idn"), R(at, 0, 512)), (R(b), R("idn"), na)])
                tt(R(at, 512, 1024), R(b), A, ALU.max)
            else:
                act(na, A, ACT.Sign)
                mm([(R(b), R("idn"), R(at, 0, 512)), (R(b), R("nk"), na)])
                act(na, R(b), ACT.Relu)
                b = bank()
                mm([(R(b), R("idn"), A), (R(b), R("idn"), na)])
                act(R(at, 512, 1024), R(b), ACT.Identity)
            if t == 1:
                send(bg, R(bg, 0, 1024), R(bgin), 2)
            if t == 0:
                for k in range(4):
                    send("tab%d" % k, R("t0", 512 * k, 512 * k + 512), R("u0", 512 * k, 512 * k + 512) if k else R("gw", 512, 1024), 1)
                    if "tab%d" % k not in RELAYED:
                        ops[-1]["after"] = ["bg0"]
            else:
                pr[0] += 3
                send("ab1", R(bg, 512, 1024), R("w1", 0, 512), -1)
                send("back0", R("raw2", 0, 512), R("back", 0, 512), -1)
                ops[-1]["after"] = ["bg1"]
                send("back1", R("raw2", 1024, 2048), R("back", 1024, 2048), -1)
                ops[-1]["after"] = ["bg1"]
                store("Y", "y0", R("back", 0, 512))

        def masks():
            zb, zab = R("zb"), R("zab")
            empty(zb, R(bgin, 0, 512))
            empty(zab, R(bgin, 512, 1024))
            if not any(PAR["clamp"]):
                return
            for out, lst, c in ((R("of"), [("n7", zaj), ("nk", zb), ("p5", zab)], 768.0),
                                (R("ll", 0, 512), [("idn", R(bgin, 0, 512)), ("p5", zaj), ("pk", zb), ("nk", zab)], -768.0),
                                (R("ll", 512, 1024), [("idn", R(ain)), ("p5", zaj), ("nk", zab)], -512.0),
                                (R("ll", 1024, 1536), [("idn", R(bgin, 512, 1024)), ("pk", zaj)], -512.0)):
                b = bank()
                mm([(R(b), R(l), r) for l, r in lst])
                act(out, R(b), ACT.Identity, bias=c)

        def step(m, d):
            lo = 512 * m
            ek, rr = R("e", lo, lo + 512), R("rr", lo, lo + 512)
            oo = 32 * m + (320 * t if d == 0 else 0)
            if d == 4 and m == 0:
                act(R("don%d" % t), IND(R("t0" if t == 0 else "raw2", 0, 2048), R("off", 0, 32)), ACT.Copy)
                if t == 1:
                    send("don", R("don1"), R("donin"), 1)
            w = 256 if PAR["hs"][d] else 512
            for c in range(0, 512, w):
                ec = R("e", lo + c, lo + c + w)
                tt(ec, IND(R(tabs[t][d], 0, 2048), R("off", oo + c // 16, oo + (c + w) // 16)),
                   R("a2e", 512 * t + c, 512 * t + c + w) if d == 0 else ec, ALU.max)
            if d < 4:
                if PAR["lv"][m] > d:
                    ts(rr, ek, 1.0 / 256, ALU.mult, 144.0 - 127.5 / 256, ALU.add)
                else:
                    act(rr, ek, ACT.Identity, bias=144.0 - 127.5 / 256, scale=1.0 / 256)

        def chain(mem):
            n, m0 = len(mem), mem[0][0]
            o, lo, hi = 32 * m0, 512 * m0, 512 * (m0 + n)
            b, st, w = bank(), 4 * n, 32 * n
            mm([(R(b, 0, w), R("idn"), R("cm", 0, w))] + [(R(b, r, w, st), R("e", lo + r, hi, st), R(mat, 144, 152)) for r in range(st)], stop=False)
            mm([(R(b, r, w, st), R("rr", lo + r, hi, st), R(mat, 152, 160)) for r in range(st)], start=False)
            hz, rep = "hz%d%d" % (n, m0 // 2), 4 // n
            ts(R("q4", o, o + w), R(b, 0, w), MAGIC, ALU.add, MAGIC, ALU.subtract)
            tt(R(hz, 16 - st, 144 - st, rep), R(b, 0, w), R("q4", o, o + w), ALU.subtract)
            mm([(R(b, 128, 128 + w), R("idn"), R("av", o, o + w))]
               + [(R(b, 128, 128 + w), R(hz, 16 - st - st * k, 144 - st - st * k), R("idn", k, 128, rep)) for k in range(rep)])
            act(R(b, 256, 256 + w), R(b, 128, 128 + w), ACT.Square)
            rows = [5 * m + d + 1 for m, d in mem]
            to_offsets(R(b, 256, 256 + w), R("ct", 32 * rows[0], 32 * rows[-1] + 32, rows[1] - rows[0]), o)
            for m, d in mem:
                if d == 3:
                    rr = R("rr", 512 * m, 512 * m + 512)
                    if PAR["rv"][m]:
                        ts(rr, rr, -144.0, ALU.add, 0.0, ALU.max)
                    else:
                        act(rr, rr, ACT.Relu, bias=-144.0)

        def verdict(m, s, ns):
            k = nblk[0] % NROT; nblk[0] += 1
            w, at = 512 // ns, done_order.index(m)
            pb = R(bank(), 0, w)
            mk = [R("mk", 1536 * k + 512 * x, 1536 * k + 512 * x + w) for x in range(3)]
            dec = [(pb, R("idn"), R("e", 512 * m + s, 512 * m + 512, ns)), (pb, R("nk"), R("rr", 512 * m + s, 512 * m + 512, ns))]
            if PAR["clamp"][at]:
                lanes = [R("ll", 512 * x + s, 512 * x + 512, ns) for x in range(3)]
                y = R("yv", 512 * k, 512 * k + w)
                mm([(pb, R("idn"), R("of", s, 512, ns))] + dec[::-1])
                if PAR["ev"][at]:
                    cp_(y, pb)
                else:
                    act(y, pb, ACT.Identity)
                for x, (a, z) in enumerate(((256.0, 768.0), (0.0, 512.0), (256.0, 512.0))):
                    ts(mk[x], y, a, ALU.max, z, ALU.min)
            else:
                lanes = [R(bgin, s, 512, ns), R(ain, s, 512, ns), R(bgin, 512 + s, 1024, ns)]
                mm(dec[::-1])
                for x, z in enumerate((R("zb", s, 512, ns), R("zaj", 512 * t + s, 512 * t + 512, ns), R("zab", s, 512, ns))):
                    tt(mk[x], pb, z, ALU.mult)
            ao = 1536 * k
            nl = PAR["la"][at] if PAR["clamp"][at] and ns == 1 else 0
            if nl:
                dadd("la%d%d" % (t, at), R("mk", ao, ao + 512 * nl), R("ll", 0, 512 * nl))
            for x in range(2, -1, -1):
                ub = R(bank(), 0, w)
                mm([(ub, qq, lanes[x])] * (x >= nl) + [(ub, qq, mk[x])])
                if x < 2 and PAR["df"][at]:
                    act(ub, ub, ACT.Abs, bias=aim)
                    tt(R("ab", ao + 512 * x, ao + 512 * x + w), R("ab", ao + 1024, ao + 1024 + w), ub, ALU.subtract)
                else:
                    act(R("ab", ao + 512 * x, ao + 512 * x + w), ub, ACT.Abs, bias=aim)
            if s == 0:
                dd[m] = bank()
            for b in range(4 // ns):
                ab = [R("ab", ao + 512 * x + b, ao + 512 * x + w, 4 // ns) for x in range(3)]
                if PAR["df"][at]:
                    for x in range(2):
                        mm([(R(dd[m], 32 - 32 * x + s + ns * b, 64 - 32 * x, 4), ab[x], R("sm", 8 - 8 * x, 16 - 8 * x))])
                else:
                    mm([(R(dd[m], s + ns * b, 64, 4), ab[x], R("sm", 32 - 16 * x, 48 - 16 * x)) for x in range(3)])
            if s == ns - 1:
                fa, wb = R("fa", 32 * m, 32 * m + 32), "wb%d" % (nd[0] % NHZ)
                if PAR["fv"]:
                    ts(fa, R(dd[m], 32, 64), 0.0, ALU.is_gt, 4.0e6, ALU.mult)
                else:
                    act(fa, R(dd[m], 32, 64), ACT.Relu, scale=4.0e6)
                tt(R(wb, 12, 140, 4), R(dd[m], 0, 32), fa, ALU.is_lt)
                if nd[0] == 7:
                    mm([(R(cb, 32 * x, 32 * x + 32), R("idn"), R("lsin%d" % t, 0, 32)) for x in range(2)], start=False, stop=False)
                mm([(R(cb, 0, 64), R("idn"), R("cm", 64, 128))] * (nd[0] == 0)
                   + [(R(cb, 0, 64), R(wb, 12 - 4 * r, 140 - 4 * r), R("pick", 64 * r, 64 * r + 64)) for r in range(4)],
                   start=nd[0] == 0, stop=nd[0] == 7)
                nd[0] += 1

        for d in range(1, 4):
            ev.append((-9 + d, d + PAR["tb"], lambda d=d: tables(d)))
        if t == 1:
            ev.append((-5, PAR["pa"] - 0.1, lambda: tables(4)))
        if t == 0:
            ev.append((29, PAR["ah"], ahead))
            ev.append((30, PAR["pro"], lambda: prologue(1)))
            ev.append((-4, PAR["f0"], lambda: first_lanes(0)))
            ev.append((31, PAR["f1"], lambda: first_lanes(1)))
        ev.append((-3, PAR["pa"], partners))
        ev.append((-2, PAR["ma"], masks))
        for p, mem in wv:
            ev.append((p + 0.001, p + PAR["ch"], lambda mem=mem: chain(mem)))
        for m in range(8):
            for d in range(5):
                ev.append((pos[m] + d, pos[m] * (PAR["s0"] if d == 0 else 1) + d, lambda m=m, d=d: step(m, d)))
            ns = PAR["ns"][done_order.index(m)]
            for s in range(ns):
                ev.append((pos[m] + 4.002, pos[m] + 4 + PAR["vo"] + 0.01 * s, lambda m=m, s=s, ns=ns: verdict(m, s, ns)))
        ev.sort(key=lambda x: x[0])
        for _, v, f in ev:
            pr[0] = P0 + v
            f()
        pr[0] = P0 + 20
        tt(R("zz", 0, 64), R(cb, 0, 64), R("base"), ALU.min)
        tt(R("zz", 64, 128), R("zz", 0, 64), R("lsin%d" % t, 32, 96), ALU.max)
        cp_(R("uo%d" % t), R("zz", 64, 128))
    send("uo", R("uo1"), R("uoin"), 1)
    pr[0] = 140
    cp_(IND(R("back", 1024, 2560), R("uoin", 0, 32)), R("donin"))
    act(R("ya"), IND(R("w1"), R("uoin", 32, 64)), ACT.Copy)
    store("S", "y1", R("ya"), 512)
    store("Y", "y2", R("back", 1024, 1536))
    store("S", "y3", R("back", 1536, 2048))
    return ops


def depend(ops):
    hist, lease = {}, {}
    for i, o in enumerate(ops):
        deps, hard = {}, set()
        acc = [(a, False) for a in o["rd"]] + [(a, True) for a in o["wr"]]
        for a, w in acc:
            for j, lo, hi, wj in hist.get(a[0], []):
                if j == i:
                    continue
                meet = lo < a[2] and a[1] < hi and (w or wj)
                if leased(a[0]):
                    if meet or ops[j]["eng"] != o["eng"] or j == lease[a[0]][0]:
                        deps[j] = deps.get(j, False) or (wj and not w)
                        if meet and o["eng"] != "P":
                            hard.add(j)
                elif meet:
                    deps[j] = deps.get(j, False) or wj
                    hard.add(j)
        for j in range(i if "after" in o else 0):
            if ops[j]["name"] in o["after"]:
                deps[j] = False
        o["hard"] = hard
        o["takes"] = None
        o["banks"] = set(a[0] for a, w in acc if leased(a[0]))
        for k in o["banks"]:
            if k not in lease:
                o["takes"] = k
            lease.setdefault(k, []).append(i)
        for a, w in acc:
            h = hist.setdefault(a[0], [])
            if w and a[3] == 1 and not leased(a[0]):
                h[:] = [x for x in h if not (a[1] <= x[1] and x[2] <= a[2])]
            h.append((i, a[1], a[2], w))
        o["deps"] = deps
    return lease


def schedule(ops, shift=None):
    if "lease" not in ops[0]:
        ops[0]["lease"] = depend(ops)
        for o in ops:
            o["base"] = (o["deps"], o["hard"])
    lease = ops[0]["lease"]
    for o in ops:
        o["deps"], o["hard"] = dict(o["base"][0]), set(o["base"][1])
    LAT = COST["lat"]
    n = len(ops)
    users = [[] for _ in range(n)]
    left = [len(o["deps"]) for o in ops]
    for i, o in enumerate(ops):
        for j in o["deps"]:
            users[j].append(i)
    below = [0.0] * n
    for i in range(n - 1, -1, -1):
        below[i] = ops[i]["cost"] + ops[i]["lat"] + LAT + max([below[u] for u in users[i]] + [0.0])
    key = [ops[i]["prio"] * PAR["w"] - PAR["cp"] * below[i] + (shift[i] if shift else 0.0) for i in range(n)]
    ready = {e: [] for e in "VSPGY"}
    rt = [0.0] * n
    for i in range(n):
        if left[i] == 0:
            ready[ops[i]["eng"]].append(i)
    free = {e: 0.0 for e in "VSPGY"}
    order = {e: [] for e in "VSPGY"}
    idle = [(0.0, b, None) for b in BANKS]
    todo = {k: len(v) for k, v in lease.items()}
    until = {k: 0.0 for k in lease}
    end, link = 0.0, [0.0, 0.0]
    for _ in range(n):
        best = None
        for e in "VSPGY":
            can = [(max(rt[i], idle[0][0]) if ops[i]["takes"] else rt[i], i) for i in ready[e] if idle or not ops[i]["takes"]]
            if not can:
                continue
            t0 = max(free[e], min(can)[0])
            r, i = min((c for c in can if c[0] <= t0 + PAR["look"]), key=lambda c: (key[c[1]], c[1]))
            t0 = max(t0, r)
            if best is None or t0 < best[0]:
                best = (t0, e, i)
        t0, e, i = best
        ready[e].remove(i)
        order[e].append(i)
        o = ops[i]
        if o["takes"]:
            _, b, before = idle.pop(0)
            MAP[o["takes"]] = b
            for j in lease.get(before, []):
                o["deps"].setdefault(j, False)
                if e != "P":
                    o["hard"].add(j)
        o["t0"] = t0
        free[e] = t0 + o["cost"]
        done = free[e] + o["lat"]
        if o["kind"] == "send":
            done = landed(o, link, free[e])
        end = max(end, done)
        for k in o["banks"]:
            todo[k] -= 1
            until[k] = max(until[k], done + LAT)
            if todo[k] == 0:
                idle.append((until[k], MAP[k], k))
                idle.sort()
        for u in users[i]:
            same = ops[u]["eng"] == e and o["kind"] == "c"
            rt[u] = max(rt[u], done + (LAT if not same else COST["own"] if i in ops[u]["hard"] else 0.0))
            left[u] -= 1
            if left[u] == 0:
                ready[ops[u]["eng"]].append(u)
    key = [o["t0"] for o in ops]
    best = None
    for _ in range(PASSES):
        order, end = forward(ops, users, key)
        if best is None or end < best[0]:
            best = (end, key)
        key = backward(ops)
    return forward(ops, users, best[1])


def slot(S, E, t, c):
    lo, hi = 0, len(E)
    while lo < hi:
        if E[(lo + hi) // 2] <= t:
            lo = (lo + hi) // 2 + 1
        else:
            hi = (lo + hi) // 2
    while lo < len(S) and S[lo] < t + c:
        t = max(t, E[lo])
        lo += 1
    S.insert(lo, t)
    E.insert(lo, t + c)
    return lo, t


def landed(o, link, t):
    k = int(o["name"] in RELAYED)
    link[k] = max(link[k], t + 5000 * k) + o["lat"] - 1800
    return link[k] + 1800 + (0 if o["name"] in ("a0", "uo") else 4000)


def wake(p, o, hard):
    return COST["lat"] if p["eng"] != o["eng"] or p["kind"] != "c" else COST["own"] if hard else 0.0


def forward(ops, users, key):
    lease = ops[0]["lease"]
    for o in ops:
        o["deps"], o["hard"] = dict(o["base"][0]), set(o["base"][1])
    left = [len(o["deps"]) for o in ops]
    rt = [0.0] * len(ops)
    ready = [i for i in range(len(ops)) if left[i] == 0]
    S, E, order = [{e: [] for e in "VSPGY"} for _ in range(3)]
    idle = [(0.0, b, None) for b in BANKS]
    todo = {k: len(v) for k, v in lease.items()}
    until = {k: 0.0 for k in lease}
    end, link = 0.0, [0.0, 0.0]
    while ready:
        i = min((j for j in ready if idle or not ops[j]["takes"]), key=lambda j: (key[j], j))
        ready.remove(i)
        o = ops[i]
        e, t = o["eng"], rt[i]
        if o["takes"]:
            can = [x for x in idle if x[0] <= t]
            x = max(can) if can else min(idle)
            idle.remove(x)
            t = max(t, x[0])
            MAP[o["takes"]] = x[1]
            for j in lease.get(x[2], []):
                o["deps"].setdefault(j, False)
                if e != "P":
                    o["hard"].add(j)
        if e in "GY" and E[e]:
            t = max(t, E[e][-1])
        k, t = slot(S[e], E[e], t, o["cost"])
        order[e].insert(k, i)
        o["t0"] = t
        done = t + o["cost"] + o["lat"]
        if o["kind"] == "send":
            done = landed(o, link, t + o["cost"])
        o["done"] = done
        end = max(end, done)
        for b in o["banks"]:
            todo[b] -= 1
            until[b] = max(until[b], done + COST["lat"])
            if todo[b] == 0:
                idle.append((until[b], MAP[b], b))
        for u in users[i]:
            rt[u] = max(rt[u], done + wake(o, ops[u], i in ops[u]["hard"]))
            left[u] -= 1
            if left[u] == 0:
                ready.append(u)
    return order, end


def backward(ops):
    left = [0] * len(ops)
    for o in ops:
        for j in o["deps"]:
            left[j] += 1
    rt = [0.0] * len(ops)
    key = [0.0] * len(ops)
    ready = [i for i in range(len(ops)) if left[i] == 0]
    S, E = [{e: [] for e in "VSPGY"} for _ in range(2)]
    while ready:
        i = min(ready, key=lambda j: (-ops[j]["done"], j))
        ready.remove(i)
        o = ops[i]
        t = slot(S[o["eng"]], E[o["eng"]], rt[i] + o["done"] - o["t0"] - o["cost"], o["cost"])[1] + o["cost"]
        key[i] = -t - (PAR["early"] if o["eng"] in "GY" else 0.0)
        for j in o["deps"]:
            rt[j] = max(rt[j], t + wake(ops[j], o, j in o["hard"]))
            left[j] -= 1
            if left[j] == 0:
                ready.append(j)
    return key


PLAN = {}


def rank_program(g, core, T, topo):
    rank = T.rank_of(core)
    cores = T.cores
    n = len(cores)
    helper = [[c for c in topo.cores_of(x) if topo.die(c) != topo.die(x)][0] for x in cores]
    if rank is None and core not in helper:
        return
    if not PLAN:
        PLAN["ops"] = build()
        PLAN["order"], PLAN["end"] = schedule(PLAN["ops"])
    ops, order = PLAN["ops"], PLAN["order"]

    def inner(r, hop):
        out = topo.engines(cores[r], cores[(r + hop) % n])
        return [x for x in topo.engines(cores[r], helper[r]) if x not in out]

    if rank is None:
        r = helper.index(core)
        for i in order["G"]:
            o = ops[i]
            if o["name"] in RELAYED:
                src, dst, hop = o["fn"]
                peer = cores[(r + hop) % n]
                rid, pid = topo.addr(peer, core)
                g.wait_ge(T.sem["r_" + o["name"]], len(inner(r, hop)))
                g.remote_dma(ap(T, dst), ap(T, dst), T.sem["r_" + o["name"]], T.sem["l_" + o["name"]], pid, rid, topo.mask(core, peer))
        for i in order["G"]:
            if ops[i]["name"] in RELAYED:
                g.wait_ge(T.sem["l_" + ops[i]["name"]], len(topo.engines(core, cores[(r + ops[i]["fn"][2]) % n])))
        return
    queue = {"V": g.vector, "S": g.scalar, "P": g.tensor, "G": g, "Y": g.sync}
    count = {}
    total = {}
    for e in "VSPG":
        k = 0
        for i in order[e]:
            if ops[i]["kind"] == "c":
                k += 1
                count[i] = k
        total["e" + e] = k
    for i, o in enumerate(ops):
        if o["kind"] == "dma":
            total["d_" + o["name"]] = 16
        elif o["kind"] == "send":
            hop = o["fn"][2]
            relayed = o["name"] in RELAYED
            total["l_" + o["name"]] = len(inner(rank, hop) if relayed else topo.engines(core, cores[(rank + hop) % n]))
            total["r_" + o["name"]] = len(topo.engines((helper if relayed else cores)[(rank - hop) % n], core))
    for e in "YSPVG":
        q = queue[e]
        seen = {}
        for i in order[e]:
            o = ops[i]
            need = {}
            for j, raw in o["deps"].items():
                p = ops[j]
                if p["kind"] == "c":
                    if p["eng"] == e and o["kind"] == "c" and j not in o["hard"]:
                        continue
                    s, v = "e" + p["eng"], count[j]
                elif p["kind"] == "dma":
                    s, v = "d_" + p["name"], 16
                else:
                    s = ("r_" if raw else "l_") + p["name"]
                    v = total[s]
                need[s] = max(need.get(s, 0), v)
            for s, v in need.items():
                if seen.get(s, 0) < v:
                    q.wait_ge(T.sem[s], v)
                    seen[s] = v
            if o["kind"] == "c":
                o["fn"](g, T).then_inc(T.sem["e" + e], 1)
            elif o["kind"] == "dma":
                o["fn"](g, T).then_inc(T.sem["d_" + o["name"]], 16)
            else:
                src, dst, hop = o["fn"]
                relayed = o["name"] in RELAYED
                peer = helper[rank] if relayed else cores[(rank + hop) % n]
                mask = sum(1 << x for x in inner(rank, hop)) if relayed else topo.mask(core, peer)
                rid, pid = topo.addr(peer, core)
                g.remote_dma(ap(T, dst), ap(T, src), T.sem["r_" + o["name"]], T.sem["l_" + o["name"]], pid, rid, mask)
        if e == "G":
            for s, v in total.items():
                if seen.get(s, 0) < v:
                    g.wait_ge(T.sem[s], v)
